import numpy as np, ml_dtypes
CORES = [1,5,17,21,33,37,49,53]
N = 8
import mx_ref
BF = ml_dtypes.bfloat16
def pick(q, e):
    c = np.concatenate([q[0].reshape(128, -1, 4), np.zeros((128, 1, 4), np.uint8)], axis=1); s = np.concatenate([q[1], np.ones((16, 1), np.uint8)], axis=1)
    return (np.ascontiguousarray(c[:, e].reshape(128, -1)), np.ascontiguousarray(s[:, e]))
def join(*qs):
    return (np.concatenate([q[0] for q in qs], axis=1), np.concatenate([q[1] for q in qs], axis=1))
def put(q, e, v):
    c, s = q[0].reshape(128, -1, 4).copy(), q[1].copy(); c[:, e] = v[0].reshape(128, -1, 4); s[:, e] = v[1]
    return (c.reshape(128, -1), s)
def pk(c, s):
    return (np.ascontiguousarray(c), mx_ref.live(s))
def emit(q):
    return q[0], q[1]
def cols(t, e):
    v = np.concatenate([t.reshape(128, -1, 4), np.zeros((128, 1, 4), BF)], axis=1)
    return np.ascontiguousarray(v[:, e]).reshape(128, -1)
def cut(t, i, w=512):
    return t[:, w * i:w * i + w]
def decode(q):
    o = []
    for b in range(4):
        e = np.zeros((128, 128, 4), np.float32); e[np.arange(128), np.arange(128), b] = 1
        o.append(mx_ref.matmul(mx_ref.quantize(e.reshape(128, 512).astype(BF)), q))
    return np.stack(o, axis=2).reshape(128, -1)
def f(rng, *shape):
    return mx_ref.flush((rng.standard_normal(shape, dtype=np.float32) * np.exp2(rng.integers(-2, 3, shape[:-1] + (1,)))).astype(BF))
def wide(rng, *shape, cols=0):
    v = rng.standard_normal(shape, dtype=np.float32) * np.exp2(rng.integers(-12, 13, shape)).astype(np.float32)
    if cols: v *= np.repeat(np.exp2(rng.integers(-cols, cols + 1, shape[:-2] + (1, shape[-1] // 4))) * (rng.random(shape[:-2] + (1, shape[-1] // 4)) > 0.0625), 4, axis=-1).astype(np.float32)
    return mx_ref.flush(v.astype(BF))
G, T, CAPP, R = 16, 96, 48, 3
def fit(v):
    v = np.array(v, np.float32)
    v[np.abs(v) < np.float32(2.0 ** -10)] = 0
    return v.astype(BF)
def plain(rng):
    return {"cb": fit(f(rng, N, 128, 4 * G)), "x": fit(f(rng, N, 128, 4 * R * T)), "w": f(rng, N, 128, 512)}
def part(rng, lab, k):
    s = (128, len(k), 4)
    v = np.where(k[None, :, None] == 2, rng.standard_normal(s), 1 + rng.random(s))
    return (v * (lab[:, None] == k[None, :])[:, :, None]).reshape(128, -1)
def setup_inputs(rng):
    return plain(rng)
def setup_inputs_crowd(rng):
    d = plain(rng)
    lab = rng.permutation(np.repeat([0, 1, 2], [40, 40, 48]))
    q, g = int(rng.integers(0, N - 2)), rng.permutation(G)[:2]
    home = int(rng.integers(0, R))
    rush = (home + 1 + int(rng.integers(0, R - 1))) % R
    cb = np.stack([part(rng, lab, np.full(G, 2)) for r in range(N)])
    k, size = np.zeros(G, int), np.full(G, 2.0 ** -6)
    k[g[1]] = 1
    size[g] = 1
    cb[q] = part(rng, lab, k) * np.repeat(size, 4)
    kinds = np.full((N, R, T), 2)
    for t in range(R):
        three, whole = np.sort(rng.permutation(N)[:3]), -1
        if t == home: three = np.concatenate([[q], np.sort(q + 1 + rng.permutation(N - 1 - q)[:2])])
        if t == rush:
            four, j = np.sort(rng.permutation(N)[:4]), int(rng.integers(0, 3))
            three, whole = np.delete(four, j), int(four[j])
        for s in range(N):
            more = int(rng.integers(1, T // 8 + 1))
            if s == three[0]: e = np.concatenate([np.zeros(CAPP, int), np.ones(more, int)])
            elif s == three[1]: e = np.concatenate([np.zeros(CAPP - 1, int), np.ones(1, int)])
            elif s == three[2]: e = np.concatenate([np.zeros(CAPP - 1, int), np.ones(1, int), rng.integers(0, 2, more)])
            elif s == whole: e = np.concatenate([np.zeros(CAPP, int), np.ones(T - CAPP, int)])
            else: e = np.zeros(int(rng.integers(CAPP // 2, CAPP + T // 8 + 1)), int)
            kinds[s, t, np.sort(rng.permutation(T)[:len(e)])] = e
    d["cb"], d["x"] = fit(cb), fit(np.stack([part(rng, lab, kinds[s].reshape(-1)) for s in range(N)]))
    return d
def setup_inputs_ties(rng):
    d = plain(rng)
    H = G // 2
    shared = fit(rng.standard_normal((128, 4 * H)))
    for r in range(N):
        both = np.concatenate([shared, fit(rng.standard_normal((128, 4 * H)))], axis=1)
        d["cb"][r] = cols(both, rng.permutation(np.concatenate([rng.integers(0, H, G - H), H + np.arange(H)])))
        v = cut(d["x"][r], 0, 4 * T).copy().reshape(128, T, 4)
        at = rng.permutation(T)
        v[:, at[:H]] = shared.reshape(128, H, 4)
        v[:, at[H:H + T // 16]] = 0
        d["x"][r] = np.concatenate([cols(v.reshape(128, -1), rng.permutation(T)) for t in range(R)], axis=1)
    return d
def setup_inputs_full(rng):
    d = plain(rng)
    at = rng.permutation(128)
    own = at[None, :] == np.arange(128)[:, None]
    cb = (1 + rng.random((128, 128, 4))) * np.where(own, 1.0, 2.0 ** -8)[:, :, None]
    kinds, who = np.zeros((N, R, T), int), np.arange(128) // G
    least, below = [], []
    for t in range(R):
        s, q = [int(v) for v in rng.permutation(N)[:2]]
        mine, free = np.flatnonzero(who == q), np.flatnonzero(who != q)
        if t == 0 or t == R - 1:
            least.append(int(rng.choice([v for v in free if G <= v < 128 - G and v not in least])))
            free = free[free != least[-1]]
            below.append((s + 1 + int(rng.integers(0, N - 1))) % N)
        for r in range(N):
            if r == s: kinds[r, t] = rng.permutation(np.concatenate([mine, mine, rng.choice(free, T - 2 * G)]))
            elif r < s: kinds[r, t] = rng.choice(free, T)
            else: kinds[r, t] = rng.choice(np.concatenate([free, mine]), T)
    x = np.zeros((N, 128, R * T, 4))
    for r in range(N):
        k = kinds[r].reshape(-1)
        x[r] = np.where(own[:, k][:, :, None], 1 + rng.random((128, R * T, 4)), (2 * rng.random((128, R * T, 4)) - 1) * 2.0 ** -7)
    x[below[0]][:, :2] = -(1 + rng.random((128, 2, 4))) * np.where(own[:, least[0]], 2.0 ** -9, 2.0 ** -6)[:, None, None]
    size = np.where(own[:, least[1]], 2.0 ** 15, np.where(own[:, least[0]], 2.0 ** 24, 2.0 ** 21))
    i = (R - 1) * T
    x[below[1]][:, i:i + 2] = -(3 + rng.random((128, 2, 4))) * size[:, None, None]
    d["cb"] = fit(np.stack([cb[:, G * r:G * r + G].reshape(128, -1) for r in range(N)]))
    d["x"] = fit(x.reshape(N, 128, -1))
    return d
def setup_inputs_idle(rng):
    d = plain(rng)
    q, own = int(rng.integers(0, N)), rng.permutation(128) < 64
    cb = rng.standard_normal((N, 128, 4 * G))
    for r in range(N): cb[r] *= (own if r == q else ~own)[:, None]
    early = np.arange(4 * R * T) < 4 * (R - 1) * T
    d["cb"], d["x"] = fit(cb), fit(d["x"].astype(np.float32) * ~(own[:, None] & early[None, :]))
    return d
def setup_inputs_spread(rng):
    d = plain(rng)
    d["cb"] = fit(wide(rng, N, 128, 4 * G).astype(np.float32) * 64)
    d["x"] = fit(wide(rng, N, 128, 4 * R * T, cols=4).astype(np.float32) * 64)
    return d
def check_inputs(d):
    b = []
    for k, lo, hi in (("cb", -10, 28), ("x", -10, 28), ("w", -30, 30)):
        v = np.abs(d[k].astype(np.float32))
        if not (np.isfinite(v).all() and ((v == 0) | (v >= 2.0 ** lo) & (v <= 2.0 ** hi)).all()): b.append("a value of " + k)
    return b
def admitted(win):
    a = np.full((2, 128), -1)
    for s in range(N):
        n = np.zeros(N, int)
        for i in range(T):
            k = win[T * s + i]
            n[k // G] += 1
            if n[k // G] > CAPP: continue
            if a[0, k] < 0: a[0, k] = T * s + i
            elif a[1, k] < 0: a[1, k] = T * s + i
    return a
def reference(cb, x, w):
    y, ids = np.zeros((N, 128, R * 2 * G), np.float32), np.zeros((N, 1, R * 2 * G), np.float32)
    oc, osc = np.zeros((N, 128, 4 * G), np.uint8), np.zeros((N, 16, G), np.uint8)
    half, quarter = np.float32(0.5), np.float32(0.25)
    qw = [mx_ref.quantize(np.ascontiguousarray(w[r])) for r in range(N)]
    c = join(*[mx_ref.quantize(np.ascontiguousarray(cb[r])) for r in range(N)])
    for t in range(R):
        tok = join(*[mx_ref.quantize(np.ascontiguousarray(cut(x[s], t, 4 * T))) for s in range(N)])
        a = admitted(np.argmax(mx_ref.matmul(c, tok) + np.float32(0), axis=0))
        for r in range(N):
            e = a[:, G * r:G * r + G].T.reshape(-1)
            i = t * 2 * G
            y[r, :, i:i + 2 * G] = mx_ref.matmul(qw[r], pick(tok, e))
            ids[r, 0, i:i + 2 * G] = e
        v = decode(join(c, pick(tok, a[0]), pick(tok, a[1]))).reshape(128, 3, 128, 4)
        one = half * v[:, 0] + half * v[:, 1]
        two = half * v[:, 0] + (quarter * v[:, 1] + quarter * v[:, 2])
        new = np.where((a[1] >= 0)[None, :, None], two, one).reshape(128, 512).astype(BF)
        moved = np.flatnonzero(a[0] >= 0)
        c = put(c, moved, pick(mx_ref.quantize(np.ascontiguousarray(new)), moved))
    for r in range(N):
        oc[r], osc[r] = emit(pick(c, np.arange(G * r, G * r + G)))
    return {"y": y, "ids": ids, "oc": oc, "osc": osc}

@@ -1,0 +1,573 @@
+from concourse.bass import DstId, RemoteDMATransfer
+from concourse.mybir import dt, AluOpType, AxisListType, ActivationFunctionType
+
+G, TOK, CAPP, R, H = 16, 96, 48, 3, 4
+TW = 544
+MARK, OWN, STEP = 12288, 80, 64
+FIRST = MARK + OWN - (STEP // 2 - (CAPP - STEP // 2))
+CO = 48
+BY0, BYH = {"c": 0, "s": 1}, {"c": 3, "s": 2}
+
+F32, BF, I32, U16, COD, PLN = "float32", "bfloat16", "int32", "uint16", "float8_e4m3fn_x4", "uint8"
+SCRATCH = {"PS": ("psum", [128, 4096], F32)}
+SEMAPHORES = ["vd", "sd", "pd", "gd", "sent"]
+
+
+def _buf(name, n, dtype):
+    SCRATCH[name] = ("sbuf", [128, n], dtype)
+
+
+def _mx(name, n):
+    _buf(name + "c", n, COD)
+    _buf(name + "s", n, PLN)
+
+
+for _n, _w in (("CBT", 512), ("X0", 512), ("X12", 768), ("WT", 512), ("ZT", 704), ("TRT", 512), ("E25", 2048), ("THR", 128), ("KP", 128),
+               ("KO", 128), ("HI", 40), ("LO", 40), ("OT", 512), ("NT", 512), ("NO", 512), ("YF", 40), ("Y", 552), ("NEW", 512), ("J", 512),
+               ("SC", 128)):
+    _buf(_n, _w, BF)
+for _n, _w in (("RM", 128), ("NEG", 128), ("DV", 128), ("TA", 256), ("QC", 1), ("KZ", 4), ("RB", 512), ("WV", 4), ("OW", 18), ("AA", 4), ("BB", 4),
+               ("CO", 2), ("FL", 12), ("TB", 4), ("TU", 2), ("HF", 2), ("TT", 4), ("IV", 4), ("UU", 8), ("UV", 2),
+               ("SS", 64), ("HB", 64), ("WN", 128), ("HC", 64), ("BQ", 4), ("YO", 96)):
+    _buf(_n, _w, F32)
+for _n, _w in (("QI", 1), ("QJ", 1), ("NJ", 6), ("NV", 120), ("RI", 128)):
+    _buf(_n, _w, I32)
+for _n, _w in (("LI", 6), ("LC", 2)):
+    _buf(_n, _w, U16)
+for _n, _w in (("XQ0", 128), ("XQ12", 192), ("WQ", 128), ("TRQ", 128), ("E25Q", 512), ("OC", 128), ("NQ", 128), ("NOQ", 128), ("YQ", 138),
+               ("HX0", 96), ("HX12", 192)):
+    _mx(_n, _w)
+for _t in range(R):
+    _mx("TK%d" % _t, TW)
+    _mx("CA%d" % _t, 128)
+    _mx("PP%d" % _t, 32)
+    _mx("PK%d" % _t, 144)
+    _buf("NP%d" % _t, 18, F32)
+    _buf("LN%d" % _t, 2, F32)
+    _buf("ID%d" % _t, 2, F32)
+    _buf("OP%d" % _t, 2, U16)
+    _buf("OF%d" % _t, 4, U16)
+    _buf("OS%d" % _t, 4, U16)
+    SEMAPHORES += ["aC%d" % _t, "aT%d" % _t, "aL%d" % _t, "aK%d" % _t, "hc%d" % _t, "hs%d" % _t, "gc%d" % _t, "gs%d" % _t]
+for _t in range(R + 1):
+    _mx("HW%d" % _t, 176)
+SEMAPHORES += ["d%d" % _i for _i in range(30)]
+
+
+def _bits(es):
+    return sum(1 << e for e in es)
+
+
+def _helper_of(core, T, topo, i):
+    return [c for c in topo.cores_of(core) if T.rank_of(c) is None and topo.die(c) == topo.die(core)][i]
+
+
+def _half(r):
+    return list(range(H * (r // H), H * (r // H) + H))
+
+
+def _base(r):
+    return 0 if r < H else 32
+
+
+def _land(r):
+    return 4 * TOK + 32 if r < H else 0
+
+
+def _dst(c, topo):
+    a = topo.addr(c)
+    return DstId(rid=a[0], pnc=a[1])
+
+
+def _relay(t):
+    return ("Q0", 0) if t == 0 else ("Q12", TOK * (t - 1))
+
+
+def _far(rank, T, topo):
+    n = len(T.cores)
+    order = [(rank + i) % n for i in range(1, n)]
+    return [r for r in order if topo.chip(T.cores[r]) != topo.chip(T.cores[rank])]
+
+
+def _near_engines(a, b, far, topo):
+    return [e for e in topo.engines(a, b) if e not in topo.engines(a, far)]
+
+
+def _hand_on(g, core, rank, T, topo, k):
+    me = T.cores[rank]
+    far = [r for r in _half(rank) if topo.chip(T.cores[r]) != topo.chip(me)]
+    es = topo.engines(core, T.cores[far[0]])
+    near = _near_engines(me, core, T.cores[far[0]], topo)
+    byt = (lambda v: v.bitcast(dt.uint8)) if k == "c" else (lambda v: v)
+    n = 0
+    for t in range(R):
+        g.wait_ge(T.sem["h%s%d" % (k, t)], len(near) if t == 0 else len(near) // 2)
+        dsts = []
+        for r in far:
+            o = _base(r) + TOK * (rank % H)
+            dsts.append(byt(T["TK%d%s" % (t, k)][:, o:o + TOK]))
+        nm, a = _relay(t)
+        g.remote_dma_fused([RemoteDMATransfer(dst_ids=[_dst(T.cores[r], topo) for r in far], dma_engine_mask=_bits(es),
+                                              remote_sem=T.sem["aT%d" % t], srcs=[byt(T["HX" + nm[1:] + k][:, a:a + TOK])], dsts=dsts)],
+                           local_sem=T.sem.sent)
+        n += len(es)
+    mate = [r for r in range(len(T.cores)) if r != rank and topo.chip(T.cores[r]) == topo.chip(me)]
+    en = _near_engines(core, T.cores[mate[0]], T.cores[far[0]], topo)
+    for t in range(1, R):
+        last = _far(rank, T, topo)[-BYH[k]:]
+        g.wait_ge(T.sem["g%s%d" % (k, t)], len(near))
+        v = byt(T["CA%d%s" % (t, k)][:, G * rank:G * rank + G])
+        g.remote_dma_fused([RemoteDMATransfer(dst_ids=[_dst(T.cores[r], topo) for r in rs], dma_engine_mask=_bits(e), remote_sem=T.sem["aC%d" % t],
+                                              srcs=[v], dsts=[v] * len(rs)) for e, rs in ((es, last), (en, mate))], local_sem=T.sem.sent)
+        n += len(es) + len(en)
+    g.wait_ge(T.sem.sent, n)
+
+
+def _first(g, core, rank, T, topo):
+    last = _far(rank, T, topo)[-BY0["s"]:]
+    es = topo.engines(core, T.cores[last[0]])
+    g.wait_ge(T.sem.gs0, len(_near_engines(T.cores[rank], core, T.cores[last[0]], topo)))
+    v = T.CA0s[:, G * rank:G * rank + G]
+    g.remote_dma_fused([RemoteDMATransfer(dst_ids=[_dst(T.cores[r], topo) for r in last], dma_engine_mask=_bits(es), remote_sem=T.sem.aC0,
+                                          srcs=[v], dsts=[v] * len(last))], local_sem=T.sem.sent)
+    g.wait_ge(T.sem.sent, len(es))
+
+
+def rank_program(g, core, T, topo):
+    rank = T.rank_of(core)
+    if rank is None:
+        for r in range(len(T.cores)):
+            for i, k in enumerate("cs"):
+                if _helper_of(T.cores[r], T, topo, i) == core:
+                    _hand_on(g, core, r, T, topo, k)
+            if _helper_of(T.cores[r], T, topo, 2) == core:
+                _first(g, core, r, T, topo)
+        return
+    AL, AF, AX = AluOpType, ActivationFunctionType, AxisListType.X
+    half, sl = rank // H, rank % H
+    part = (rank + H) % (2 * H)
+    both = (rank, part)
+    tb, lb = _base(rank), _land(rank)
+    z = tb + 4 * TOK
+    on1, ln1 = (H * TOK + 1, 2 * H * TOK + 1) if half == 0 else (2 * H * TOK + 1, H * TOK + 1)
+    eng = {"v": g.vector, "s": g.scalar, "p": g.tensor, "g": g, "y": g.sync}
+    done = {"v": "vd", "s": "sd", "p": "pd", "g": "gd"}
+    cnt, seen, log, nd = {}, {}, {}, [0]
+
+    def cols(x):
+        nm, a, b = x[0], x[1], x[2]
+        st = x[3] if len(x) > 3 else 1
+        if nm == "PS":
+            return nm, frozenset(range(a // 512, (b - 1) // 512 + 1))
+        return nm, frozenset(range(a, b, st))
+
+    def view(x):
+        st = x[3] if len(x) > 3 else 1
+        return T[x[0]][:, x[1]:x[2]] if st == 1 else T[x[0]][:, x[1]:x[2]:st]
+
+    def wait(q, tok):
+        if seen.get((q, tok[0]), 0) < tok[1]:
+            eng[q].wait_ge(T.sem[tok[0]], tok[1])
+            seen[(q, tok[0])] = tok[1]
+
+    def before(q, rd, wr):
+        best = {}
+        for kind, xs in (("r", rd), ("w", wr)):
+            for x in xs:
+                nm, cs = cols(x)
+                for k, c2, tok, q2 in log.get(nm, []):
+                    if (kind == "w" or k == "w") and cs & c2 and not (q == "p" and q2 == "p"):
+                        best[tok[0]] = max(best.get(tok[0], 0), tok[1])
+        for s in sorted(best):
+            wait(q, (s, best[s]))
+
+    def after(q, tok, rd, wr):
+        for x in wr:
+            nm, cs = cols(x)
+            log[nm] = [e for e in log.get(nm, []) if not e[1] <= cs] + [("w", cs, tok, q)]
+        for x in rd:
+            nm, cs = cols(x)
+            log.setdefault(nm, []).append(("r", cs, tok, q))
+
+    def op(q, f, rd, wr):
+        before(q, rd, wr)
+        cnt[q] = cnt.get(q, 0) + 1
+        tok = (done[q], cnt[q])
+        f(eng[q]).then_inc(T.sem[tok[0]], 1)
+        after(q, tok, rd, wr)
+        return tok
+
+    def isap(x):
+        return isinstance(x, tuple)
+
+    def ts(out, in0, s1, op0, s2=None, op1=None):
+        sc = [view(s) if isap(s) else s for s in (s1, s2)]
+        rd = [in0] + [s for s in (s1, s2) if isap(s)]
+        if op1 is None:
+            return op("v", lambda v: v.tensor_scalar(view(out), view(in0), sc[0], None, op0), rd, [out])
+        return op("v", lambda v: v.tensor_scalar(view(out), view(in0), sc[0], sc[1], op0, op1), rd, [out])
+
+    def tt(out, a, b, o):
+        return op("v", lambda v: v.tensor_tensor(view(out), view(a), view(b), o), [a, b], [out])
+
+    def cp(out, a):
+        return op("v", lambda v: v.tensor_copy(view(out), view(a)), [a], [out])
+
+    def act(out, a, f, bias=0.0, scale=1.0, acc=None):
+        rd = [a] + [x for x in (bias, scale) if isap(x)]
+        b, c = [view(x) if isap(x) else x for x in (bias, scale)]
+        if acc is not None:
+            return op("s", lambda s: s.activation(view(out), view(a), f, bias=b, scale=c, accum_out=view(acc)), rd, [out, acc])
+        if f == AF.Copy:
+            return op("s", lambda s: s.activation(view(out), view(a), f, scale=c), rd, [out])
+        return op("s", lambda s: s.activation(view(out), view(a), f, bias=b, scale=c), rd, [out])
+
+    def fill(x, c):
+        return op("v", lambda v: v.memset(view(x), c), [], [x])
+
+    def scan(out, d0, d1, ini, o0, o1):
+        return op("v", lambda v: v.tensor_tensor_scan(view(out), view(d0), view(d1), ini, o0, o1), [d0, d1], [out])
+
+    def top2(nm, x):
+        scan((nm, 0, 17, 2), x, ("NEG", 0, 9), 0.0, AL.max, AL.max)
+        scan((nm, 3, 18, 2), (x[0], x[1] + 1, x[2]), (nm, 0, 15, 2), 0.0, AL.max, AL.min)
+
+    def qz(nm, a, n, tile, ta=0):
+        oc, os, i = (nm + "c", a, a + n), (nm + "s", a, a + n), (tile, ta, ta + 4 * n)
+        return op("v", lambda v: v.quantize_mx(view(oc), view(os), view(i)), [i], [oc, os])
+
+    def mm(bank, st, sa, mv, ma, start=True, stop=True):
+        o = ("PS", 512 * bank, 512 * bank + 128)
+        a, b = (st + "c", sa, sa + 128), (st + "s", sa, sa + 128)
+        c, d = (mv + "c", ma, ma + 128), (mv + "s", ma, ma + 128)
+        return op("p", lambda p: p.matmul_mx(view(o), view(a), view(b), view(c), view(d), start, stop), [a, b, c, d], [o])
+
+    def pick(dst, da, src, wa, wb, of, oa, ob):
+        n = 16 * (ob - oa)
+        o, w, f = (of, oa, ob), (src + "c", wa, wb), (dst + "c", da, da + n)
+        op("v", lambda v: v.tensor_copy(view(f).bitcast(dt.uint32), view(w).bitcast(dt.uint32).indirect(view(o))), [w, o], [f])
+        w2, f2 = (src + "s", wa, wb), (dst + "s", da, da + n)
+        op("s", lambda s: s.activation(view(f2), view(w2).indirect(view(o)), AF.Copy), [w2, o], [f2])
+
+    def dma(q, out, in_, rd, wr):
+        before(q, rd, wr)
+        tok = ("d%d" % nd[0], 16)
+        nd[0] += 1
+        eng[q].dma_start(out, in_).then_inc(T.sem[tok[0]], 16)
+        after(q, tok, rd, wr)
+
+    def iota(x, pat, base, ch):
+        if SCRATCH[x[0]][2] == I32:
+            op("g", lambda e: e.iota(view(x), pat, base, ch), [], [x])
+        else:
+            op("g", lambda e: e.iota(view(x), pat, base, ch, allow_small_or_imprecise_dtypes=True), [], [x])
+
+    def ext(sem, val, xs):
+        for x in xs:
+            nm, cs = cols(x)
+            log.setdefault(nm, []).append(("w", cs, (sem, val), "x"))
+
+    peers = [r for r in range(len(T.cores)) if r != rank]
+    near = [r for r in peers if topo.chip(T.cores[r]) == topo.chip(core)]
+    far = _far(rank, T, topo)
+    efar = topo.engines(core, T.cores[far[0]])
+    enear = _near_engines(core, T.cores[near[0]], T.cores[far[0]], topo)
+    hn2 = len(enear) // 2
+    hand = {"c": _helper_of(core, T, topo, 0), "s": _helper_of(core, T, topo, 1)}
+    sent = [0]
+
+    def send(transfers):
+        tr, rd = [], []
+        for es, sem, src, dsts in transfers:
+            code = SCRATCH[src[0]][2] == COD
+            b = (lambda v: v.bitcast(dt.uint8)) if code else (lambda v: v)
+            tr.append(RemoteDMATransfer(dst_ids=[_dst(c, topo) for c, _ in dsts], dma_engine_mask=_bits(es), remote_sem=T.sem[sem],
+                                        srcs=[b(view(src))], dsts=[b(view(x)) for _, x in dsts]))
+            rd.append(src)
+            sent[0] += len(es)
+        before("g", rd, [])
+        g.remote_dma_fused(tr, local_sem=T.sem.sent)
+
+    def spread(t, k, es, to):
+        src = ("HW%d%s" % (t, k), CO, CO + G)
+        x = ("CA%d%s" % (t, k), G * rank, G * rank + G)
+        direct = len(far) - (BY0[k] if t == 0 else BYH[k])
+        tr = []
+        if es[0]:
+            tr.append((es[0], "aC%d" % t, src, [(T.cores[r], x) for r in far[:direct]]))
+        if es[1]:
+            tr.append((es[1], "aC%d" % t if to == "mate" else "g%s%d" % (k, t), src, [(T.cores[near[0]] if to == "mate" else to, x)]))
+        send(tr)
+
+    def tokens(t, k, es):
+        nm, a = _relay(t)
+        src = ("X" + nm + k, a, a + TOK)
+        o = tb + TOK * sl
+        tr = []
+        if es[0]:
+            tr.append((es[0], "h%s%d" % (k, t), src, [(hand[k], ("HX" + nm[1:] + k, a, a + TOK))]))
+        if es[1]:
+            tr.append((es[1], "aT%d" % t, src, [(T.cores[r], ("TK%d%s" % (t, k), o, o + TOK)) for r in near]))
+        send(tr)
+
+    dma("y", T.CBT[:, 0:4 * G], T.cb[:], [], [("CBT", 0, 4 * G)])
+    dma("s", T.X0[:, 0:4 * TOK], T.x[:, 0:4 * TOK], [], [("X0", 0, 4 * TOK)])
+    dma("y", T.X12[:], T.x[:, 4 * TOK:12 * TOK], [], [("X12", 0, 8 * TOK)])
+    dma("s", T.WT[:], T.w[:], [], [("WT", 0, 512)])
+    iota(("DV", 0, 128), [[1, 128]], 0, -1)
+    iota(("QI", 0, 1), [[0, 1]], 0, 1)
+    iota(("NJ", 0, 6), [[16, 6]], 0, 0)
+    iota(("NV", 0, 40), [[0, 10], [TOK, 4]], TOK, -1)
+    fill(("CBT", 4 * G, 512), 0.0)
+    fill(("ZT", 0, 704), 0.0)
+    for t in range(R):
+        qz("TK%d" % t, tb + 4 * TOK, 128, "ZT")
+    qz("HW0", 0, 128, "ZT")
+    fill(("X0", 4 * TOK, 512), 0.0)
+    qz("XQ0", 0, 128, "X0")
+    qz("HW0", CO, 128, "CBT")
+    for k in "cs":
+        tokens(0, k, [enear, []])
+    spread(0, "c", [efar, []], None)
+    spread(0, "s", [efar, enear], _helper_of(core, T, topo, 2))
+    for k in "cs":
+        spread(0, k, [[], enear], "mate")
+    for k in "cs":
+        tokens(0, k, [[], enear])
+    qz("XQ12", 0, 2 * TOK, "X12")
+    for t in range(1, R):
+        for k in "cs":
+            tokens(t, k, [enear[hn2:], enear[:hn2]])
+    camec = 2 * (len(efar) * len(far) + len(enear) * len(near))
+    for t in range(R):
+        came = 2 * (len(enear) if t == 0 else hn2) + 2 * len(efar) * len([r for r in _half(rank) if r in far])
+        for s in range(H):
+            if s != sl:
+                ext("aT%d" % t, came, [("TK%d%s" % (t, k), tb + TOK * s, tb + TOK * s + TOK) for k in "cs"])
+        for r in peers:
+            ext("aC%d" % t, camec, [("CA%d%s" % (t, k), G * r, G * r + G) for k in "cs"])
+        ext("aK%d" % t, 2 * len(efar), [("TK%d%s" % (t, k), lb, lb + 32) for k in "cs"])
+        ext("aL%d" % t, len(efar), [("LN%d" % t, 0, 2)])
+
+    dv, ta, tc = ("DV", 0, 128), ("TA", 0, 128), ("TA", 128, 256)
+    for b in range(4):
+        act(("E25", 512 * b, 512 * b + 512), ("ZT", 0, 512), AF.Copy)
+    act(("NEG", 0, 128), ("ZT", 0, 128), AF.Identity, bias=-1e29)
+    act(("YF", 0, 40), ("ZT", 0, 40), AF.Copy)
+    for e in range(2):
+        iota(("THR", 64 * e, 64 * e + 64), [[1, G], [1, 4]], G * both[e], 0)
+    iota(("KP", 0, 128), [[0, 8], [1, 16]], G * part, 0)
+    iota(("RI", 0, 128), [[0, 4], [1, 32]], 0, 0)
+    iota(("KO", 0, 128), [[0, 8], [1, 16]], G * rank, 0)
+    for e in range(2):
+        for i in range(2):
+            iota(("THR", 64 * e + 2 + i, 64 * e + 64, 4), [[0, G]], G * (both[e] + i), 0)
+    ts(ta, dv, 1.0, AL.is_ge, -128.0, AL.mult)
+    ts(tc, dv, 0.0, AL.is_equal, float(MARK), AL.mult)
+    tt(ta, ta, tc, AL.add)
+    ts(("TRT", 2, 512, 4), ta, 1.0 / 128, AL.mult, float(OWN), AL.min)
+    act(("TRT", 3, 512, 4), ("TRT", 2, 512, 4), AF.Copy, scale=-1.0)
+    act(("TRT", 0, 512, 4), ta, AF.Copy)
+    act(("TRT", 1, 512, 4), ta, AF.Copy, scale=-1.0)
+    for b in range(4):
+        ts(("E25", 512 * b + b, 512 * b + 512, 4), dv, 0.0, AL.is_equal, 0.25, AL.mult)
+    ts(("QJ", 0, 1), ("QI", 0, 1), 15, AL.bitwise_and)
+    cp(("QC", 0, 1), ("QJ", 0, 1))
+    ts(("LI", 0, 6), ("NJ", 0, 6), ("QC", 0, 1), AL.add)
+    ts(("LC", 0, 1), ("QC", 0, 1), float(CO), AL.add)
+    pick("CA0", G * rank, "HW0", 0, 64 + G, "LC", 0, 1)
+    for t in range(R):
+        nm, a = _relay(t)
+        pick("TK%d" % t, tb + TOK * sl, "X" + nm, a, a + TOK, "LI", 0, 6)
+    ts(("RM", 0, 128), ("RI", 0, 128), 0.5, AL.is_ge)
+    fill(("TRT", 4 * TOK, 512), 0.0)
+    op("v", lambda v: v.memset(T.TRT[TOK:128, :], 0.0), [], [("TRT", 0, 512)])
+    qz("TRQ", 0, 128, "TRT")
+    ts(("NV", 40, 80), ("NV", 0, 40), 16.0, AL.add)
+    ts(("NV", 80, 120), ("NV", 40, 80), 5, AL.arith_shift_right)
+    ts(("HI", 0, 40), ("NV", 80, 120), 32.0, AL.mult)
+    tt(("LO", 0, 40), ("NV", 0, 40), ("HI", 0, 40), AL.subtract)
+    for i, c in enumerate((lb - z, lb + 16 - z, lb)):
+        act(("KZ", i, i + 1), ("QC", 0, 1), AF.Identity, bias=float(c))
+    act(("Y", 80, 552), ("ZT", 0, 472), AF.Copy)
+    for b in range(4):
+        act(("BQ", b, b + 1), ("QC", 0, 1), AF.Identity, bias=float(16 * b))
+        act(("WN", 64 + 16 * b, 80 + 16 * b), ("CBT", b, 64, 4), AF.Copy)
+    qz("HW1", 0, 128, "ZT")
+    qz("PK0", 0, 144, "ZT")
+    qz("E25Q", 0, 512, "E25")
+
+    def score(s):
+        r = ("RB", 128 * s, 128 * s + 128)
+        scan(r, ("PS", 512 * s, 512 * s + 128), ("NEG", 0, 128), -1e29, AL.max, AL.max)
+        act(("J", 128 * s, 128 * s + 128), r, AF.Sign, bias=("RB", 128 * s + 127, 128 * s + 128), scale=-1.0, acc=("WV", s, s + 1))
+
+    def thr(s):
+        ts(("OT", 128 * s, 128 * s + 128), ("THR", 0, 128), ("WV", s, s + 1), AL.is_le)
+
+    def hot(s):
+        ts(("NT", s, 512, 4), ("KP", 0, 128), ("WV", s, s + 1), AL.is_equal)
+
+    def mine(s):
+        ts(("NO", s, 512, 4), ("KO", 0, 128), ("WV", s, s + 1), AL.is_equal)
+
+    for t in range(R):
+        tk, ca, pp, pk, hw, hn = "TK%d" % t, "CA%d" % t, "PP%d" % t, "PK%d" % t, "HW%d" % t, "HW%d" % (t + 1)
+        np_, ln, final = "NP%d" % t, "LN%d" % t, t + 1 == R
+        for s in range(H):
+            mm(s, tk, tb + TOK * (H - 1 - s), ca, 0)
+        for f, s in ((score, 0), (score, 1), (score, 2), (thr, 0), (score, 3), (thr, 1), (thr, 2), (hot, 0), (hot, 1), (thr, 3)):
+            f(s)
+        qz("OC", 0, 128, "OT")
+        mm(4, "TRQ", 0, "OC", 0)
+        hot(2)
+        hot(3)
+        qz("NQ", 0, 128, "NT")
+        if t == 0:
+            act(("NEW", 64, 512), ("ZT", 0, 448), AF.Copy)
+        mk = ("SC", 31, 128, 32)
+        scan(("SC", 0, 128), ("RM", 0, 128), ("PS", 2048, 2176), 0.0, AL.mult, AL.max)
+        mine(0)
+        for i in range(2):
+            ts(("YF", 20 * i, 20 * i + 20, 5), mk, float(FIRST - 128 * i), AL.is_equal)
+        mine(1)
+        tt(("Y", 0, 40), ("YF", 0, 40), ("HI", 0, 40), AL.mult)
+        tt(("Y", 40, 80), ("YF", 0, 40), ("LO", 0, 40), AL.mult)
+        mine(2)
+        qz("YQ", 0, 138, "Y")
+        mm(5, "NQ", 0, "YQ", 0, True, False)
+        mm(5, "NQ", 0, "YQ", 10, False, True)
+        mine(3)
+        qz("NOQ", 0, 128, "NO")
+        mm(6, "NOQ", 0, "YQ", 0, True, False)
+        mm(6, "NOQ", 0, "YQ", 10, False, True)
+        top2(np_, ("PS", 2560, 2569))
+        ts(("OP%d" % t, 0, 2), (np_, 16, 18), -1.0, AL.mult, float(4 * TOK), AL.add)
+        send([(efar, "aL%d" % t, (np_, 16, 18), [(T.cores[part], (ln, 0, 2))])])
+        pick(pp, 0, tk, tb, (lb if half == 0 else TW), "OP%d" % t, 0, 2)
+        for k in "cs":
+            send([(efar, "aK%d" % t, (pp + k, 0, 32), [(T.cores[part], (tk + k, _land(part), _land(part) + 32))])])
+        top2("OW", ("PS", 3072, 3081))
+        n1, n2, n12 = ("OW", 16, 17), ("OW", 17, 18), ("OW", 16, 18)
+        k1z, k2z, k1 = ("KZ", 0, 1), ("KZ", 1, 2), ("KZ", 2, 3)
+        b0, b1, b2, c1, c2 = ("BB", 0, 1), ("BB", 1, 2), ("BB", 2, 3), ("CO", 0, 1), ("CO", 1, 2)
+        fl = [("FL", i, i + 1) for i in range(12)]
+        ts(("AA", 0, 3, 2), n12, -1.0, AL.mult, float(z), AL.add)
+        ts(fl[0], n2, 0.5, AL.is_lt, n1, AL.mult)
+        if half == 0:
+            ts(b0, n1, 0.5, AL.is_lt, k1z, AL.mult)
+            ts(fl[1], n2, 0.5, AL.is_lt, k1z, AL.mult)
+            ts(("AA", 1, 2), fl[0], -1.0, AL.mult, ("AA", 2, 3), AL.add)
+            ts(c1, n1, 0.5, AL.is_lt, 16.0, AL.mult)
+            ts(b1, fl[1], fl[0], AL.add)
+            ts(b2, fl[1], b0, AL.subtract)
+            ts(c2, n1, 0.5, AL.is_lt, k2z, AL.mult)
+        else:
+            ts(b0, n1, k1z, AL.add)
+            ts(b2, n2, n1, AL.subtract)
+            ts(("AA", 1, 2), fl[0], -1.0, AL.mult, ("AA", 2, 3), AL.add)
+            ts(fl[1], n1, 0.5, AL.is_ge, b0, AL.mult)
+            ts(c2, b0, 16.0, AL.add)
+            ts(fl[2], fl[1], -1.0, AL.mult, k1, AL.add)
+            ts(c1, fl[1], 16.0, AL.add)
+            ts(b1, fl[2], ("AA", 1, 2), AL.subtract)
+        ts(fl[3], n1, 0.5, AL.is_lt, 64.0, AL.mult)
+        v1, v2, v12 = ("IV", 0, 1), ("IV", 1, 2), ("IV", 0, 2)
+        ts(("IV", 2, 4), n12, 0.5, AL.is_ge, float(on1), AL.mult)
+        if half == 0:
+            ts(fl[4], n1, 0.5, AL.is_lt)
+            ts(fl[5], n2, 0.5, AL.is_lt, fl[4], AL.subtract)
+        tt(v12, ("IV", 2, 4), n12, AL.subtract)
+        if half == 1:
+            ts(fl[4], v1, v2, AL.subtract)
+        for b in range(4):
+            mm(7, "E25Q", 128 * b, hw, CO - 16 * b, b == 0, b == 3)
+        act(("WN", 0, 64), ("PS", 3584, 3584 + 64), AF.Copy, scale=2.0)
+        h1, h2, of = ("HF", 0, 1), ("HF", 1, 2), "OF%d" % t
+        ts(("HF", 0, 2), (ln, 0, 2), 0.5, AL.is_ge)
+        ts(("TB", 0, 3), ("BB", 0, 3), h1, AL.mult)
+        ts(("TU", 0, 2), ("CO", 0, 2), h2, AL.mult)
+        ts((of, 0, 1), ("AA", 0, 1), ("TB", 0, 1), AL.add)
+        for i in range(2):
+            ts((of, 1 + i, 2 + i), ("AA", 1 + i, 2 + i), ("TB", 1 + i, 2 + i), AL.add, ("TU", i, i + 1), AL.add)
+
+        def lin(out, a, scale, bias):
+            act(out, a, AF.Identity, bias=bias, scale=scale)
+
+        u = [("UU", i, i + 1) for i in range(8)]
+
+        def number0():
+            lin(("UU", 0, 2), (ln, 0, 2), -1.0, float(ln1))
+            if half == 1:
+                lin(("UU", 6, 8), ("HF", 0, 2), -1.0, 1.0)
+            lin(u[2], u[0], h1, 0.0)
+            lin(u[3], u[1], h2, 0.0)
+
+        def number1():
+            if half == 0:
+                lin(u[5], u[2], fl[5], v2)
+                lin(("UV", 0, 1), u[2], fl[4], v1)
+                lin(("UV", 1, 2), u[3], fl[4], u[5])
+            else:
+                lin(u[5], h1, fl[4], v2)
+                lin(("UV", 0, 1), v1, u[6], u[2])
+                lin(("UV", 1, 2), u[5], u[7], u[3])
+            lin(("ID%d" % t, 0, 2), ("UV", 0, 2), 1.0, -1.0)
+
+        def store_ids():
+            dma("y", T.ids[:, 32 * t:32 * t + 32], T["ID%d" % t][0:16, 0:2], [("ID%d" % t, 0, 2)], [])
+
+        if final:
+            number0()
+        pick(pk, 0, tk, 0, TW, "OF%d" % t, 0, 3)
+        for b in range(3):
+            mm(b, "E25Q", 128 * b, pk, 0)
+        mm(3, "E25Q", 384, pk, 16, True, False)
+        mm(3, "E25Q", 384, pk, 0, False, True)
+        ts(("TT", 1, 2), h1, 0.5, AL.is_lt, fl[3], AL.mult)
+        ts(("OS%d" % t, 0, 4), ("BQ", 0, 4), ("TT", 1, 2), AL.add)
+        w, o, h = ("WN", 0, 128), ("OS%d" % t, 0, 4), ("HC", 0, 64)
+        op("s", lambda q, w=w, o=o, h=h: q.activation(view(h), view(w).indirect(view(o)), AF.Copy), [w, o], [h])
+        for f, b in (("h", 0), ("h", 1), ("n", 0), ("h", 2), ("n", 1), ("n", 2), ("n", 3)):
+            c, h = 16 * b, ("PS", 512 * b, 512 * b + 16)
+            if f == "h":
+                act(("SS", c, c + 16), ("PS", 512 * b + 16, 512 * b + 32), AF.Copy)
+                tt(("HB", c, c + 16), h, ("SS", c, c + 16), AL.add)
+            else:
+                tt(("NEW", b, 64, 4), h if b == 3 else ("HB", c, c + 16), ("HC", c, c + 16), AL.add)
+        qz(hn, CO, 128, "NEW")
+        if not final:
+            for k in "cs":
+                spread(t + 1, k, [efar, enear], hand[k])
+            pick("CA%d" % (t + 1), G * rank, hn, 0, 64 + G, "LC", 0, 1)
+            for b in range(4):
+                act(("WN", 64 + 16 * b, 80 + 16 * b), ("NEW", b, 64, 4), AF.Copy)
+        if t == 0:
+            qz("WQ", 0, 128, "WT")
+        if not final:
+            qz("PK%d" % (t + 1), 0, 144, "ZT")
+            qz("HW%d" % (t + 2), 0, 128, "ZT")
+        mm(6, "WQ", 0, pk, 0)
+        if final:
+            number1()
+            store_ids()
+        for i in range(2):
+            act(("YO", 32 * t + i, 32 * t + 32, 2), ("PS", 3072 + 32 * i, 3072 + 32 * i + 16), AF.Copy)
+        if final:
+            i = (hn + "c", CO, CO + G)
+            dma("y", T.oc[:, 0:4 * G], view(i).bitcast(dt.uint8), [i], [])
+        else:
+            number0()
+            number1()
+            wait("y", ("aC%d" % (t + 1), camec))
+            store_ids()
+        dma("s" if final else "y", T.y[:, 32 * t:32 * t + 32], T.YO[:, 32 * t:32 * t + 32], [("YO", 32 * t, 32 * t + 32)], [])
+        if final:
+            for k in range(4):
+                dma("ys"[k % 2], T.osc[4 * k:4 * k + 4, 0:G], T[hn + "s"][32 * k:32 * k + 4, CO:CO + G], [(hn + "s", CO, CO + G)], [])
+
+    for q in cnt:
+        wait("g", (done[q], cnt[q]))
+    for i in range(nd[0]):
+        wait("g", ("d%d" % i, 16))
+    g.wait_ge(T.sem.sent, sent[0])

@@ -1,16 +1,15 @@
 from concourse.bass import DstId, RemoteDMATransfer
 from concourse.mybir import dt, AluOpType, AxisListType, ActivationFunctionType
 
-G, TOK, CAPP, R, H = 16, 96, 48, 3, 4
-TW = 544
-MARK, OWN, STEP = 12288, 80, 64
-FIRST = MARK + OWN - (STEP // 2 - (CAPP - STEP // 2))
-CO = 48
-BY0, BYH = {"c": 0, "s": 1}, {"c": 3, "s": 2}
+G, TOK, CAPP, R, NR = 16, 96, 48, 3, 8
+NB = TOK // G
+Z = 128 * NR
+BIG = 2048.0
+CA_ = 128
 
 F32, BF, I32, U16, COD, PLN = "float32", "bfloat16", "int32", "uint16", "float8_e4m3fn_x4", "uint8"
 SCRATCH = {"PS": ("psum", [128, 4096], F32)}
-SEMAPHORES = ["vd", "sd", "pd", "gd", "sent"]
+SEMAPHORES = ["vd", "sd", "pd", "gd", "sent", "aC", "hc0", "hs0", "hc1", "hs1"]
 
 
 def _buf(name, n, dtype):
@@ -22,36 +21,33 @@ def _mx(name, n):
     _buf(name + "s", n, PLN)
 
 
-for _n, _w in (("CBT", 512), ("X0", 512), ("X12", 768), ("WT", 512), ("ZT", 704), ("TRT", 512), ("E25", 2048), ("THR", 128), ("KP", 128),
-               ("KO", 128), ("HI", 40), ("LO", 40), ("OT", 512), ("NT", 512), ("NO", 512), ("YF", 40), ("Y", 552), ("NEW", 512), ("J", 512),
-               ("SC", 128)):
+for _n, _w in (("CBT", 512), ("X0", 512), ("X12", 896), ("WT", 512), ("ZT", 512), ("E25", 2048), ("NEW", 512), ("J", 40 * NB)):
     _buf(_n, _w, BF)
-for _n, _w in (("RM", 128), ("NEG", 128), ("DV", 128), ("TA", 256), ("QC", 1), ("KZ", 4), ("RB", 512), ("WV", 4), ("OW", 18), ("AA", 4), ("BB", 4),
-               ("CO", 2), ("FL", 12), ("TB", 4), ("TU", 2), ("HF", 2), ("TT", 4), ("IV", 4), ("UU", 8), ("UV", 2),
-               ("SS", 64), ("HB", 64), ("WN", 128), ("HC", 64), ("BQ", 4), ("YO", 96)):
+for _n, _w in (("NEG", 128), ("DV", 128), ("QC", 1), ("PF", 1), ("VC", 1), ("WI", 40), ("TH", 80), ("TO", 80), ("VAL", 96), ("RB", 136 * NB),
+               ("WL", 8), ("CP", 40), ("HV", 192), ("OG", 208), ("TT", 2), ("CAP", 192), ("SB", 32 * 97), ("Y1", 32), ("Y2", 64), ("RR", 256),
+               ("KK", 2), ("FF", 2), ("IB", 4), ("SS", 64), ("HB", 64), ("WN", 256), ("HC", 64), ("BQ", 4), ("YO", 96), ("YS", 144)):
     _buf(_n, _w, F32)
-for _n, _w in (("QI", 1), ("QJ", 1), ("NJ", 6), ("NV", 120), ("RI", 128)):
+for _n, _w in (("QI", 1), ("QJ", 1), ("RI", 48), ("IA", 4)):
     _buf(_n, _w, I32)
-for _n, _w in (("LI", 6), ("LC", 2)):
+for _n, _w in (("RL", 48), ("LC", 2), ("DL", 4), ("IX", 6), ("OS", 4), ("YL", 2)):
     _buf(_n, _w, U16)
-for _n, _w in (("XQ0", 128), ("XQ12", 192), ("WQ", 128), ("TRQ", 128), ("E25Q", 512), ("OC", 128), ("NQ", 128), ("NOQ", 128), ("YQ", 138),
-               ("HX0", 96), ("HX12", 192)):
+for _n, _w in (("XQ", 192), ("WQ", 128), ("E25Q", 512), ("CA", 128), ("RP", 128 * NB)):
     _mx(_n, _w)
 for _t in range(R):
-    _mx("TK%d" % _t, TW)
-    _mx("CA%d" % _t, 128)
-    _mx("PP%d" % _t, 32)
-    _mx("PK%d" % _t, 144)
-    _buf("NP%d" % _t, 18, F32)
+    _mx("TK%d" % _t, Z + 128)
+    _mx("PM%d" % _t, 32)
+    _mx("PK%d" % _t, 160)
+    _buf("NM%d" % _t, 36, F32)
+    _buf("NO%d" % _t, 36, F32)
     _buf("LN%d" % _t, 2, F32)
     _buf("ID%d" % _t, 2, F32)
-    _buf("OP%d" % _t, 2, U16)
+    _buf("MX%d" % _t, 8, F32)
+    _buf("MR%d" % _t, 24, F32)
     _buf("OF%d" % _t, 4, U16)
-    _buf("OS%d" % _t, 4, U16)
-    SEMAPHORES += ["aC%d" % _t, "aT%d" % _t, "aL%d" % _t, "aK%d" % _t, "hc%d" % _t, "hs%d" % _t, "gc%d" % _t, "gs%d" % _t]
+    SEMAPHORES += ["aTc%d" % _t, "aTs%d" % _t, "aL%d" % _t, "aK%d" % _t, "aM%d" % _t, "aN%d" % _t]
 for _t in range(R + 1):
-    _mx("HW%d" % _t, 176)
-SEMAPHORES += ["d%d" % _i for _i in range(30)]
+    _mx("CM%d" % _t, 288)
+SEMAPHORES += ["d%d" % _i for _i in range(24)]
 
 
 def _bits(es):
@@ -62,31 +58,22 @@ def _helper_of(core, T, topo, i):
     return [c for c in topo.cores_of(core) if T.rank_of(c) is None and topo.die(c) == topo.die(core)][i]
 
 
-def _half(r):
-    return list(range(H * (r // H), H * (r // H) + H))
-
-
-def _base(r):
-    return 0 if r < H else 32
-
-
-def _land(r):
-    return 4 * TOK + 32 if r < H else 0
-
-
 def _dst(c, topo):
     a = topo.addr(c)
     return DstId(rid=a[0], pnc=a[1])
 
 
-def _relay(t):
-    return ("Q0", 0) if t == 0 else ("Q12", TOK * (t - 1))
+def _pair(rank, T, topo):
+    return [r for r in range(len(T.cores)) if topo.chip(T.cores[r]) == topo.chip(T.cores[rank])]
 
 
-def _far(rank, T, topo):
+def _scorers(t, T, topo):
+    return [r for r in range(len(T.cores)) if _pair(r, T, topo)[t % 2] == r]
+
+
+def _far(rank, t, T, topo):
     n = len(T.cores)
-    order = [(rank + i) % n for i in range(1, n)]
-    return [r for r in order if topo.chip(T.cores[r]) != topo.chip(T.cores[rank])]
+    return [r for r in [(rank + i) % n for i in range(1, n)] if r in _scorers(t, T, topo) and r not in _pair(rank, T, topo)]
 
 
 def _near_engines(a, b, far, topo):
@@ -95,42 +82,27 @@ def _near_engines(a, b, far, topo):
 
 def _hand_on(g, core, rank, T, topo, k):
     me = T.cores[rank]
-    far = [r for r in _half(rank) if topo.chip(T.cores[r]) != topo.chip(me)]
-    es = topo.engines(core, T.cores[far[0]])
-    near = _near_engines(me, core, T.cores[far[0]], topo)
+    other = T.cores[_far(rank, 0, T, topo)[0]]
+    es, en = topo.engines(core, other), _near_engines(core, me, other, topo)
+    came = len(_near_engines(me, core, other, topo))
     byt = (lambda v: v.bitcast(dt.uint8)) if k == "c" else (lambda v: v)
-    n = 0
-    for t in range(R):
-        g.wait_ge(T.sem["h%s%d" % (k, t)], len(near) if t == 0 else len(near) // 2)
-        dsts = []
-        for r in far:
-            o = _base(r) + TOK * (rank % H)
-            dsts.append(byt(T["TK%d%s" % (t, k)][:, o:o + TOK]))
-        nm, a = _relay(t)
-        g.remote_dma_fused([RemoteDMATransfer(dst_ids=[_dst(T.cores[r], topo) for r in far], dma_engine_mask=_bits(es),
-                                              remote_sem=T.sem["aT%d" % t], srcs=[byt(T["HX" + nm[1:] + k][:, a:a + TOK])], dsts=dsts)],
-                           local_sem=T.sem.sent)
-        n += len(es)
-    mate = [r for r in range(len(T.cores)) if r != rank and topo.chip(T.cores[r]) == topo.chip(me)]
-    en = _near_engines(core, T.cores[mate[0]], T.cores[far[0]], topo)
+    pair = _pair(rank, T, topo)
+    n = [0]
+
+    def on(t, sem, src, dst):
+        sets = [(es, _far(rank, t, T, topo))] + ([(en, [pair[t % 2]])] if pair[t % 2] != rank else [])
+        g.remote_dma_fused([RemoteDMATransfer(dst_ids=[_dst(T.cores[r], topo) for r in rs], dma_engine_mask=_bits(e), remote_sem=T.sem[sem],
+                                              srcs=[byt(src)], dsts=[byt(dst)] * len(rs)) for e, rs in sets], local_sem=T.sem.sent)
+        n[0] += sum(len(e) for e, _ in sets)
+
+    o = CA_ + G * pair.index(rank)
+    g.wait_ge(T.sem["h%s0" % k], came)
+    on(0, "aC", T["CM0" + k][:, o:o + G], T["CA" + k][:, G * rank:G * rank + G])
+    g.wait_ge(T.sem.sent, n[0])
+    g.wait_ge(T.sem["h%s1" % k], came)
     for t in range(1, R):
-        last = _far(rank, T, topo)[-BYH[k]:]
-        g.wait_ge(T.sem["g%s%d" % (k, t)], len(near))
-        v = byt(T["CA%d%s" % (t, k)][:, G * rank:G * rank + G])
-        g.remote_dma_fused([RemoteDMATransfer(dst_ids=[_dst(T.cores[r], topo) for r in rs], dma_engine_mask=_bits(e), remote_sem=T.sem["aC%d" % t],
-                                              srcs=[v], dsts=[v] * len(rs)) for e, rs in ((es, last), (en, mate))], local_sem=T.sem.sent)
-        n += len(es) + len(en)
-    g.wait_ge(T.sem.sent, n)
-
-
-def _first(g, core, rank, T, topo):
-    last = _far(rank, T, topo)[-BY0["s"]:]
-    es = topo.engines(core, T.cores[last[0]])
-    g.wait_ge(T.sem.gs0, len(_near_engines(T.cores[rank], core, T.cores[last[0]], topo)))
-    v = T.CA0s[:, G * rank:G * rank + G]
-    g.remote_dma_fused([RemoteDMATransfer(dst_ids=[_dst(T.cores[r], topo) for r in last], dma_engine_mask=_bits(es), remote_sem=T.sem.aC0,
-                                          srcs=[v], dsts=[v] * len(last))], local_sem=T.sem.sent)
-    g.wait_ge(T.sem.sent, len(es))
+        on(t, "aT%s%d" % (k, t), T["XQ" + k][:, TOK * (t - 1):TOK * t], T["TK%d%s" % (t, k)][:, 128 * rank:128 * rank + TOK])
+    g.wait_ge(T.sem.sent, n[0])
 
 
 def rank_program(g, core, T, topo):
@@ -140,16 +112,14 @@ def rank_program(g, core, T, topo):
             for i, k in enumerate("cs"):
                 if _helper_of(T.cores[r], T, topo, i) == core:
                     _hand_on(g, core, r, T, topo, k)
-            if _helper_of(T.cores[r], T, topo, 2) == core:
-                _first(g, core, r, T, topo)
         return
     AL, AF, AX = AluOpType, ActivationFunctionType, AxisListType.X
-    half, sl = rank // H, rank % H
-    part = (rank + H) % (2 * H)
-    both = (rank, part)
-    tb, lb = _base(rank), _land(rank)
-    z = tb + 4 * TOK
-    on1, ln1 = (H * TOK + 1, 2 * H * TOK + 1) if half == 0 else (2 * H * TOK + 1, H * TOK + 1)
+    pair = _pair(rank, T, topo)
+    me = pair.index(rank)
+    mate = pair[1 - me]
+    co = CA_ + G * me
+    q0 = co + G - 128 if me == 0 else co
+    e0 = 4 * (co - q0)
     eng = {"v": g.vector, "s": g.scalar, "p": g.tensor, "g": g, "y": g.sync}
     done = {"v": "vd", "s": "sd", "p": "pd", "g": "gd"}
     cnt, seen, log, nd = {}, {}, {}, [0]
@@ -159,10 +129,14 @@ def rank_program(g, core, T, topo):
         st = x[3] if len(x) > 3 else 1
         if nm == "PS":
             return nm, frozenset(range(a // 512, (b - 1) // 512 + 1))
-        return nm, frozenset(range(a, b, st))
+        qs = range(x[4] // 32, x[5] // 32) if len(x) > 4 else range(4)
+        return nm, frozenset(4 * c + u for c in range(a, b, st) for u in qs)
 
     def view(x):
         st = x[3] if len(x) > 3 else 1
+        p0, p1 = (x[4], x[5]) if len(x) > 4 else (0, 128)
+        if len(x) > 4:
+            return T[x[0]][p0:p1, x[1]:x[2]:st]
         return T[x[0]][:, x[1]:x[2]] if st == 1 else T[x[0]][:, x[1]:x[2]:st]
 
     def wait(q, tok):
@@ -176,7 +150,8 @@ def rank_program(g, core, T, topo):
             for x in xs:
                 nm, cs = cols(x)
                 for k, c2, tok, q2 in log.get(nm, []):
-                    if (kind == "w" or k == "w") and cs & c2 and not (q == "p" and q2 == "p"):
+                    clash = kind == "w" or k == "w" or (nm == "PS" and q2 != q)
+                    if clash and cs & c2 and not (q == "p" and q2 == "p"):
                         best[tok[0]] = max(best.get(tok[0], 0), tok[1])
         for s in sorted(best):
             wait(q, (s, best[s]))
@@ -222,19 +197,24 @@ def rank_program(g, core, T, topo):
             return op("s", lambda s: s.activation(view(out), view(a), f, scale=c), rd, [out])
         return op("s", lambda s: s.activation(view(out), view(a), f, bias=b, scale=c), rd, [out])
 
+    def take(q, out, win, of):
+        if q == "v":
+            return op("v", lambda v: v.tensor_copy(view(out), view(win).indirect(view(of))), [win, of], [out])
+        return op("s", lambda s: s.activation(view(out), view(win).indirect(view(of)), AF.Copy), [win, of], [out])
+
     def fill(x, c):
         return op("v", lambda v: v.memset(view(x), c), [], [x])
 
     def scan(out, d0, d1, ini, o0, o1):
-        return op("v", lambda v: v.tensor_tensor_scan(view(out), view(d0), view(d1), ini, o0, o1), [d0, d1], [out])
+        i = view(ini) if isap(ini) else ini
+        return op("v", lambda v: v.tensor_tensor_scan(view(out), view(d0), view(d1), i, o0, o1), [d0, d1] + ([ini] if isap(ini) else []), [out])
 
-    def top2(nm, x):
-        scan((nm, 0, 17, 2), x, ("NEG", 0, 9), 0.0, AL.max, AL.max)
-        scan((nm, 3, 18, 2), (x[0], x[1] + 1, x[2]), (nm, 0, 15, 2), 0.0, AL.max, AL.min)
+    def turn(out, a):
+        return op("v", lambda v: v.transpose(view(out), view(a)), [a], [out])
 
     def qz(nm, a, n, tile, ta=0):
-        oc, os, i = (nm + "c", a, a + n), (nm + "s", a, a + n), (tile, ta, ta + 4 * n)
-        return op("v", lambda v: v.quantize_mx(view(oc), view(os), view(i)), [i], [oc, os])
+        oc, os_, i = (nm + "c", a, a + n), (nm + "s", a, a + n), (tile, ta, ta + 4 * n)
+        return op("v", lambda v: v.quantize_mx(view(oc), view(os_), view(i)), [i], [oc, os_])
 
     def mm(bank, st, sa, mv, ma, start=True, stop=True):
         o = ("PS", 512 * bank, 512 * bank + 128)
@@ -242,12 +222,16 @@ def rank_program(g, core, T, topo):
         c, d = (mv + "c", ma, ma + 128), (mv + "s", ma, ma + 128)
         return op("p", lambda p: p.matmul_mx(view(o), view(a), view(b), view(c), view(d), start, stop), [a, b, c, d], [o])
 
-    def pick(dst, da, src, wa, wb, of, oa, ob):
-        n = 16 * (ob - oa)
-        o, w, f = (of, oa, ob), (src + "c", wa, wb), (dst + "c", da, da + n)
+    def pickc(dst, da, src, wa, wb, of, oa, ob):
+        o, w, f = (of, oa, ob), (src + "c", wa, wb), (dst + "c", da, da + 16 * (ob - oa))
         op("v", lambda v: v.tensor_copy(view(f).bitcast(dt.uint32), view(w).bitcast(dt.uint32).indirect(view(o))), [w, o], [f])
-        w2, f2 = (src + "s", wa, wb), (dst + "s", da, da + n)
-        op("s", lambda s: s.activation(view(f2), view(w2).indirect(view(o)), AF.Copy), [w2, o], [f2])
+
+    def picks(q, dst, da, src, wa, wb, of, oa, ob):
+        take(q, (dst + "s", da, da + 16 * (ob - oa)), (src + "s", wa, wb), (of, oa, ob))
+
+    def pick(dst, da, src, wa, wb, of, oa, ob):
+        pickc(dst, da, src, wa, wb, of, oa, ob)
+        picks("s", dst, da, src, wa, wb, of, oa, ob)
 
     def dma(q, out, in_, rd, wr):
         before(q, rd, wr)
@@ -262,17 +246,18 @@ def rank_program(g, core, T, topo):
         else:
             op("g", lambda e: e.iota(view(x), pat, base, ch, allow_small_or_imprecise_dtypes=True), [], [x])
 
+    outer = []
+
     def ext(sem, val, xs):
+        outer.append((sem, val))
         for x in xs:
             nm, cs = cols(x)
             log.setdefault(nm, []).append(("w", cs, (sem, val), "x"))
 
-    peers = [r for r in range(len(T.cores)) if r != rank]
-    near = [r for r in peers if topo.chip(T.cores[r]) == topo.chip(core)]
-    far = _far(rank, T, topo)
-    efar = topo.engines(core, T.cores[far[0]])
-    enear = _near_engines(core, T.cores[near[0]], T.cores[far[0]], topo)
-    hn2 = len(enear) // 2
+    peers = [r for r in range(NR) if r != rank]
+    other = T.cores[_far(rank, 0, T, topo)[0]]
+    efar, eall = topo.engines(core, other), topo.engines(core, T.cores[mate])
+    enear = _near_engines(core, T.cores[mate], other, topo)
     hand = {"c": _helper_of(core, T, topo, 0), "s": _helper_of(core, T, topo, 1)}
     sent = [0]
 
@@ -288,286 +273,261 @@ def rank_program(g, core, T, topo):
         before("g", rd, [])
         g.remote_dma_fused(tr, local_sem=T.sem.sent)
 
-    def spread(t, k, es, to):
-        src = ("HW%d%s" % (t, k), CO, CO + G)
-        x = ("CA%d%s" % (t, k), G * rank, G * rank + G)
-        direct = len(far) - (BY0[k] if t == 0 else BYH[k])
-        tr = []
-        if es[0]:
-            tr.append((es[0], "aC%d" % t, src, [(T.cores[r], x) for r in far[:direct]]))
-        if es[1]:
-            tr.append((es[1], "aC%d" % t if to == "mate" else "g%s%d" % (k, t), src, [(T.cores[near[0]] if to == "mate" else to, x)]))
-        send(tr)
-
-    def tokens(t, k, es):
-        nm, a = _relay(t)
-        src = ("X" + nm + k, a, a + TOK)
-        o = tb + TOK * sl
-        tr = []
-        if es[0]:
-            tr.append((es[0], "h%s%d" % (k, t), src, [(hand[k], ("HX" + nm[1:] + k, a, a + TOK))]))
-        if es[1]:
-            tr.append((es[1], "aT%d" % t, src, [(T.cores[r], ("TK%d%s" % (t, k), o, o + TOK)) for r in near]))
-        send(tr)
-
-    dma("y", T.CBT[:, 0:4 * G], T.cb[:], [], [("CBT", 0, 4 * G)])
+    dma("y", T.CBT[:, e0:e0 + 4 * G], T.cb[:], [], [("CBT", e0, e0 + 4 * G)])
     dma("s", T.X0[:, 0:4 * TOK], T.x[:, 0:4 * TOK], [], [("X0", 0, 4 * TOK)])
-    dma("y", T.X12[:], T.x[:, 4 * TOK:12 * TOK], [], [("X12", 0, 8 * TOK)])
+    dma("y", T.X12[:, 0:8 * TOK], T.x[:, 4 * TOK:12 * TOK], [], [("X12", 0, 8 * TOK)])
     dma("s", T.WT[:], T.w[:], [], [("WT", 0, 512)])
     iota(("DV", 0, 128), [[1, 128]], 0, -1)
     iota(("QI", 0, 1), [[0, 1]], 0, 1)
-    iota(("NJ", 0, 6), [[16, 6]], 0, 0)
-    iota(("NV", 0, 40), [[0, 10], [TOK, 4]], TOK, -1)
-    fill(("CBT", 4 * G, 512), 0.0)
-    fill(("ZT", 0, 704), 0.0)
-    for t in range(R):
-        qz("TK%d" % t, tb + 4 * TOK, 128, "ZT")
-    qz("HW0", 0, 128, "ZT")
+    iota(("RI", 0, 48), [[-G, NB], [128, NR]], TOK - 1, 0)
+    rest = (0, e0) if me == 0 else (4 * G, 512)
+    fill(("CBT",) + rest, 0.0)
     fill(("X0", 4 * TOK, 512), 0.0)
-    qz("XQ0", 0, 128, "X0")
-    qz("HW0", CO, 128, "CBT")
+    fill(("ZT", 0, 512), 0.0)
+    fill(("X12", 8 * TOK, 896), 0.0)
+    qz("CM0", q0, 128, "CBT")
+    qz("TK0", 128 * rank, 128, "X0")
     for k in "cs":
-        tokens(0, k, [enear, []])
-    spread(0, "c", [efar, []], None)
-    spread(0, "s", [efar, enear], _helper_of(core, T, topo, 2))
+        x = ("CM0" + k, co, co + G)
+        send([(enear, "h%s0" % k, x, [(hand[k], x)])])
     for k in "cs":
-        spread(0, k, [[], enear], "mate")
+        x = ("TK0" + k, 128 * rank, 128 * rank + TOK)
+        send([(efar, "aT%s0" % k, x, [(T.cores[r], x) for r in _far(rank, 0, T, topo)])] +
+             ([(enear, "aT%s0" % k, x, [(T.cores[mate], x)])] if me == 1 else []))
+    qz("XQ", 0, 2 * TOK, "X12")
     for k in "cs":
-        tokens(0, k, [[], enear])
-    qz("XQ12", 0, 2 * TOK, "X12")
-    for t in range(1, R):
-        for k in "cs":
-            tokens(t, k, [enear[hn2:], enear[:hn2]])
-    camec = 2 * (len(efar) * len(far) + len(enear) * len(near))
+        x = ("XQ" + k, 0, 2 * TOK)
+        send([(enear, "h%s1" % k, x, [(hand[k], x)])])
+    came = len(efar) * (NR - 2) + len(enear)
     for t in range(R):
-        came = 2 * (len(enear) if t == 0 else hn2) + 2 * len(efar) * len([r for r in _half(rank) if r in far])
-        for s in range(H):
-            if s != sl:
-                ext("aT%d" % t, came, [("TK%d%s" % (t, k), tb + TOK * s, tb + TOK * s + TOK) for k in "cs"])
-        for r in peers:
-            ext("aC%d" % t, camec, [("CA%d%s" % (t, k), G * r, G * r + G) for k in "cs"])
-        ext("aK%d" % t, 2 * len(efar), [("TK%d%s" % (t, k), lb, lb + 32) for k in "cs"])
-        ext("aL%d" % t, len(efar), [("LN%d" % t, 0, 2)])
+        if t % 2 == me:
+            for k in "cs":
+                ext("aT%s%d" % (k, t), came, [("TK%d%s" % (t, k), 128 * r, 128 * r + TOK) for r in peers])
+            if t == 0:
+                ext("aC", 2 * came, [("CA" + k, G * r, G * r + G) for k in "cs" for r in peers])
+            else:
+                ext("aM%d" % t, 3 * len(efar), [("MR%d" % t, 8 * i, 8 * i + NB) for i in range(3)])
+                o = CA_ + G * (1 - me)
+                ext("aN%d" % t, 2 * len(eall), [("CM%d%s" % (t, k), o, o + G) for k in "cs"])
+        else:
+            ext("aL%d" % t, len(eall), [("LN%d" % t, 0, 2)])
+            ext("aK%d" % t, 2 * len(eall), [("PK%d%s" % (t, k), 0, 32) for k in "cs"])
 
-    dv, ta, tc = ("DV", 0, 128), ("TA", 0, 128), ("TA", 128, 256)
+    dv, qc = ("DV", 0, 128), ("QC", 0, 1)
     for b in range(4):
         act(("E25", 512 * b, 512 * b + 512), ("ZT", 0, 512), AF.Copy)
     act(("NEG", 0, 128), ("ZT", 0, 128), AF.Identity, bias=-1e29)
-    act(("YF", 0, 40), ("ZT", 0, 40), AF.Copy)
-    for e in range(2):
-        iota(("THR", 64 * e, 64 * e + 64), [[1, G], [1, 4]], G * both[e], 0)
-    iota(("KP", 0, 128), [[0, 8], [1, 16]], G * part, 0)
-    iota(("RI", 0, 128), [[0, 4], [1, 32]], 0, 0)
-    iota(("KO", 0, 128), [[0, 8], [1, 16]], G * rank, 0)
-    for e in range(2):
-        for i in range(2):
-            iota(("THR", 64 * e + 2 + i, 64 * e + 64, 4), [[0, G]], G * (both[e] + i), 0)
-    ts(ta, dv, 1.0, AL.is_ge, -128.0, AL.mult)
-    ts(tc, dv, 0.0, AL.is_equal, float(MARK), AL.mult)
-    tt(ta, ta, tc, AL.add)
-    ts(("TRT", 2, 512, 4), ta, 1.0 / 128, AL.mult, float(OWN), AL.min)
-    act(("TRT", 3, 512, 4), ("TRT", 2, 512, 4), AF.Copy, scale=-1.0)
-    act(("TRT", 0, 512, 4), ta, AF.Copy)
-    act(("TRT", 1, 512, 4), ta, AF.Copy, scale=-1.0)
+    act(("WN", 128, 256), ("ZT", 0, 128), AF.Copy)
+    act(("YS", 16, 144), ("ZT", 0, 128), AF.Copy)
+    act(("NEW",) + rest, ("ZT",) + rest, AF.Copy)
+    ts(("QJ", 0, 1), ("QI", 0, 1), 15, AL.bitwise_and)
+    cp(("PF", 0, 1), ("QI", 0, 1))
+    cp(qc, ("QJ", 0, 1))
+    fill(("TO", 0, 80), 0.0)
+    ts(("WI", 0, 40), ("DV", 0, 40), ("PF", 0, 1), AL.add)
+    ts(("RL", 0, 48), ("RI", 0, 48), qc, AL.subtract)
+    ts(("LC", 0, 1), qc, 0.0, AL.add)
+    ts(("VC", 0, 1), qc, -8.0, AL.mult, float(TOK - 1 - Z), AL.add)
+    for o in range(2):
+        fill(("TO", 40 * o + 1 + G * o, 40 * o + 1 + G * o + G), BIG)
+        ts(("TH", 40 * o, 40 * o + 40), ("WI", 0, 40), qc, AL.subtract, float(1 + G * o), AL.is_equal)
+        ts(("DL", 2 * o, 2 * o + 2), ("ZT", 0, 2), qc, AL.add, float(G * o), AL.add)
+    ts(("VC", 0, 1), ("PF", 0, 1), 7.0, AL.mult, ("VC", 0, 1), AL.add)
+    if me == 0:
+        pick("CA", G * rank, "CM0", CA_, CA_ + G, "LC", 0, 1)
+    fill(("OG", 0, 208, 104), (CAPP + 1) * BIG)
+    fill(("RB", 0, 136 * NB, 136), -1e29)
+    ts(("VAL", 0, TOK), ("DV", 0, TOK), -1.0, AL.mult, ("VC", 0, 1), AL.add)
+    fill(("SB", 0, 32), 0.0)
+    fill(("SB", 32 * TOK, 32 * TOK + 32), 0.0)
+    for t in range(R):
+        if t % 2 == me:
+            fill(("NM%d" % t, 0, 1), 0.0)
+            fill(("NO%d" % t, 0, 1), 0.0)
     for b in range(4):
         ts(("E25", 512 * b + b, 512 * b + 512, 4), dv, 0.0, AL.is_equal, 0.25, AL.mult)
-    ts(("QJ", 0, 1), ("QI", 0, 1), 15, AL.bitwise_and)
-    cp(("QC", 0, 1), ("QJ", 0, 1))
-    ts(("LI", 0, 6), ("NJ", 0, 6), ("QC", 0, 1), AL.add)
-    ts(("LC", 0, 1), ("QC", 0, 1), float(CO), AL.add)
-    pick("CA0", G * rank, "HW0", 0, 64 + G, "LC", 0, 1)
-    for t in range(R):
-        nm, a = _relay(t)
-        pick("TK%d" % t, tb + TOK * sl, "X" + nm, a, a + TOK, "LI", 0, 6)
-    ts(("RM", 0, 128), ("RI", 0, 128), 0.5, AL.is_ge)
-    fill(("TRT", 4 * TOK, 512), 0.0)
-    op("v", lambda v: v.memset(T.TRT[TOK:128, :], 0.0), [], [("TRT", 0, 512)])
-    qz("TRQ", 0, 128, "TRT")
-    ts(("NV", 40, 80), ("NV", 0, 40), 16.0, AL.add)
-    ts(("NV", 80, 120), ("NV", 40, 80), 5, AL.arith_shift_right)
-    ts(("HI", 0, 40), ("NV", 80, 120), 32.0, AL.mult)
-    tt(("LO", 0, 40), ("NV", 0, 40), ("HI", 0, 40), AL.subtract)
-    for i, c in enumerate((lb - z, lb + 16 - z, lb)):
-        act(("KZ", i, i + 1), ("QC", 0, 1), AF.Identity, bias=float(c))
-    act(("Y", 80, 552), ("ZT", 0, 472), AF.Copy)
-    for b in range(4):
-        act(("BQ", b, b + 1), ("QC", 0, 1), AF.Identity, bias=float(16 * b))
-        act(("WN", 64 + 16 * b, 80 + 16 * b), ("CBT", b, 64, 4), AF.Copy)
-    qz("HW1", 0, 128, "ZT")
-    qz("PK0", 0, 144, "ZT")
-    qz("E25Q", 0, 512, "E25")
+        act(("BQ", b, b + 1), qc, AF.Identity, bias=float(32 * b + G * me))
 
-    def score(s):
-        r = ("RB", 128 * s, 128 * s + 128)
-        scan(r, ("PS", 512 * s, 512 * s + 128), ("NEG", 0, 128), -1e29, AL.max, AL.max)
-        act(("J", 128 * s, 128 * s + 128), r, AF.Sign, bias=("RB", 128 * s + 127, 128 * s + 128), scale=-1.0, acc=("WV", s, s + 1))
+    def blank(t):
+        lands = t > 0 and t % 2 == me
+        qz("CM%d" % t, (CA_ + 2 * G if lands else CA_ + G) if me == 0 else (0 if lands else G), 128, "ZT")
+        qz("PK%d" % t, 32, 128, "ZT")
+        if t % 2 == me:
+            qz("TK%d" % t, Z, 128, "ZT")
 
-    def thr(s):
-        ts(("OT", 128 * s, 128 * s + 128), ("THR", 0, 128), ("WV", s, s + 1), AL.is_le)
-
-    def hot(s):
-        ts(("NT", s, 512, 4), ("KP", 0, 128), ("WV", s, s + 1), AL.is_equal)
-
-    def mine(s):
-        ts(("NO", s, 512, 4), ("KO", 0, 128), ("WV", s, s + 1), AL.is_equal)
-
-    for t in range(R):
-        tk, ca, pp, pk, hw, hn = "TK%d" % t, "CA%d" % t, "PP%d" % t, "PK%d" % t, "HW%d" % t, "HW%d" % (t + 1)
-        np_, ln, final = "NP%d" % t, "LN%d" % t, t + 1 == R
-        for s in range(H):
-            mm(s, tk, tb + TOK * (H - 1 - s), ca, 0)
-        for f, s in ((score, 0), (score, 1), (score, 2), (thr, 0), (score, 3), (thr, 1), (thr, 2), (hot, 0), (hot, 1), (thr, 3)):
-            f(s)
-        qz("OC", 0, 128, "OT")
-        mm(4, "TRQ", 0, "OC", 0)
-        hot(2)
-        hot(3)
-        qz("NQ", 0, 128, "NT")
-        if t == 0:
-            act(("NEW", 64, 512), ("ZT", 0, 448), AF.Copy)
-        mk = ("SC", 31, 128, 32)
-        scan(("SC", 0, 128), ("RM", 0, 128), ("PS", 2048, 2176), 0.0, AL.mult, AL.max)
-        mine(0)
-        for i in range(2):
-            ts(("YF", 20 * i, 20 * i + 20, 5), mk, float(FIRST - 128 * i), AL.is_equal)
-        mine(1)
-        tt(("Y", 0, 40), ("YF", 0, 40), ("HI", 0, 40), AL.mult)
-        tt(("Y", 40, 80), ("YF", 0, 40), ("LO", 0, 40), AL.mult)
-        mine(2)
-        qz("YQ", 0, 138, "Y")
-        mm(5, "NQ", 0, "YQ", 0, True, False)
-        mm(5, "NQ", 0, "YQ", 10, False, True)
-        mine(3)
-        qz("NOQ", 0, 128, "NO")
-        mm(6, "NOQ", 0, "YQ", 0, True, False)
-        mm(6, "NOQ", 0, "YQ", 10, False, True)
-        top2(np_, ("PS", 2560, 2569))
-        ts(("OP%d" % t, 0, 2), (np_, 16, 18), -1.0, AL.mult, float(4 * TOK), AL.add)
-        send([(efar, "aL%d" % t, (np_, 16, 18), [(T.cores[part], (ln, 0, 2))])])
-        pick(pp, 0, tk, tb, (lb if half == 0 else TW), "OP%d" % t, 0, 2)
-        for k in "cs":
-            send([(efar, "aK%d" % t, (pp + k, 0, 32), [(T.cores[part], (tk + k, _land(part), _land(part) + 32))])])
-        top2("OW", ("PS", 3072, 3081))
-        n1, n2, n12 = ("OW", 16, 17), ("OW", 17, 18), ("OW", 16, 18)
-        k1z, k2z, k1 = ("KZ", 0, 1), ("KZ", 1, 2), ("KZ", 2, 3)
-        b0, b1, b2, c1, c2 = ("BB", 0, 1), ("BB", 1, 2), ("BB", 2, 3), ("CO", 0, 1), ("CO", 1, 2)
-        fl = [("FL", i, i + 1) for i in range(12)]
-        ts(("AA", 0, 3, 2), n12, -1.0, AL.mult, float(z), AL.add)
-        ts(fl[0], n2, 0.5, AL.is_lt, n1, AL.mult)
-        if half == 0:
-            ts(b0, n1, 0.5, AL.is_lt, k1z, AL.mult)
-            ts(fl[1], n2, 0.5, AL.is_lt, k1z, AL.mult)
-            ts(("AA", 1, 2), fl[0], -1.0, AL.mult, ("AA", 2, 3), AL.add)
-            ts(c1, n1, 0.5, AL.is_lt, 16.0, AL.mult)
-            ts(b1, fl[1], fl[0], AL.add)
-            ts(b2, fl[1], b0, AL.subtract)
-            ts(c2, n1, 0.5, AL.is_lt, k2z, AL.mult)
-        else:
-            ts(b0, n1, k1z, AL.add)
-            ts(b2, n2, n1, AL.subtract)
-            ts(("AA", 1, 2), fl[0], -1.0, AL.mult, ("AA", 2, 3), AL.add)
-            ts(fl[1], n1, 0.5, AL.is_ge, b0, AL.mult)
-            ts(c2, b0, 16.0, AL.add)
-            ts(fl[2], fl[1], -1.0, AL.mult, k1, AL.add)
-            ts(c1, fl[1], 16.0, AL.add)
-            ts(b1, fl[2], ("AA", 1, 2), AL.subtract)
-        ts(fl[3], n1, 0.5, AL.is_lt, 64.0, AL.mult)
-        v1, v2, v12 = ("IV", 0, 1), ("IV", 1, 2), ("IV", 0, 2)
-        ts(("IV", 2, 4), n12, 0.5, AL.is_ge, float(on1), AL.mult)
-        if half == 0:
-            ts(fl[4], n1, 0.5, AL.is_lt)
-            ts(fl[5], n2, 0.5, AL.is_lt, fl[4], AL.subtract)
-        tt(v12, ("IV", 2, 4), n12, AL.subtract)
-        if half == 1:
-            ts(fl[4], v1, v2, AL.subtract)
+    def old(t):
         for b in range(4):
-            mm(7, "E25Q", 128 * b, hw, CO - 16 * b, b == 0, b == 3)
-        act(("WN", 0, 64), ("PS", 3584, 3584 + 64), AF.Copy, scale=2.0)
-        h1, h2, of = ("HF", 0, 1), ("HF", 1, 2), "OF%d" % t
-        ts(("HF", 0, 2), (ln, 0, 2), 0.5, AL.is_ge)
-        ts(("TB", 0, 3), ("BB", 0, 3), h1, AL.mult)
-        ts(("TU", 0, 2), ("CO", 0, 2), h2, AL.mult)
-        ts((of, 0, 1), ("AA", 0, 1), ("TB", 0, 1), AL.add)
+            mm(6, "E25Q", 128 * b, "CM%d" % t, CA_ - 32 * b, b == 0, b == 3)
+        act(("WN", 0, 128), ("PS", 3072, 3200), AF.Copy, scale=2.0)
+        for b in range(4):
+            c = 128 + 32 * b + G * me
+            act(("WN", c, c + G), ("CBT" if t == 0 else "NEW", e0 + b, e0 + 64, 4), AF.Copy)
+
+    blank(0)
+    qz("E25Q", 0, 512, "E25")
+    qz("WQ", 0, 128, "WT")
+    old(0)
+
+    def flags(n):
+        ts(("FF", 0, 2), n, -0.5, AL.is_gt, 128.0, AL.mult)
+        ts(("OS", 0, 4), ("BQ", 0, 4), ("FF", 0, 1), AL.add)
+        take("s", ("HC", 0, 64), ("WN", 0, 256), ("OS", 0, 4))
+
+    def numbers(t, n):
+        ts(("IA", 0, 2), n, float(Z), AL.add)
+        ts(("YL", 0, 1), qc, ("FF", 1, 2), AL.add)
+        ts(("IA", 2, 4), ("IA", 0, 2), 7, AL.arith_shift_right)
+        ts(("IB", 0, 2), ("IA", 2, 4), float(TOK - 128), AL.mult, float(Z), AL.add)
+        tt(("IB", 2, 4), ("IB", 0, 2), n, AL.add)
         for i in range(2):
-            ts((of, 1 + i, 2 + i), ("AA", 1 + i, 2 + i), ("TB", 1 + i, 2 + i), AL.add, ("TU", i, i + 1), AL.add)
+            ts(("ID%d" % t, i, i + 1), ("FF", i, i + 1), -(NR * TOK + 1) / 128.0, AL.mult, ("IB", 2 + i, 3 + i), AL.add)
+        dma("y", T.ids[:, 32 * t:32 * t + 32], T["ID%d" % t][0:16, 0:2], [("ID%d" % t, 0, 2)], [])
 
-        def lin(out, a, scale, bias):
-            act(out, a, AF.Identity, bias=bias, scale=scale)
+    def results(t, q):
+        act(("YS", 0, G), ("PS", 3584 + G, 3584 + 2 * G), AF.Copy)
+        act(("YO", 32 * t, 32 * t + 32, 2), ("PS", 3584, 3584 + G), AF.Copy)
+        take("s", ("YO", 32 * t + 1, 32 * t + 32, 2), ("YS", 0, 144), ("YL", 0, 1))
+        dma(q, T.y[:, 32 * t:32 * t + 32], T.YO[:, 32 * t:32 * t + 32], [("YO", 32 * t, 32 * t + 32)], [])
 
-        u = [("UU", i, i + 1) for i in range(8)]
-
-        def number0():
-            lin(("UU", 0, 2), (ln, 0, 2), -1.0, float(ln1))
-            if half == 1:
-                lin(("UU", 6, 8), ("HF", 0, 2), -1.0, 1.0)
-            lin(u[2], u[0], h1, 0.0)
-            lin(u[3], u[1], h2, 0.0)
-
-        def number1():
-            if half == 0:
-                lin(u[5], u[2], fl[5], v2)
-                lin(("UV", 0, 1), u[2], fl[4], v1)
-                lin(("UV", 1, 2), u[3], fl[4], u[5])
-            else:
-                lin(u[5], h1, fl[4], v2)
-                lin(("UV", 0, 1), v1, u[6], u[2])
-                lin(("UV", 1, 2), u[5], u[7], u[3])
-            lin(("ID%d" % t, 0, 2), ("UV", 0, 2), 1.0, -1.0)
-
-        def store_ids():
-            dma("y", T.ids[:, 32 * t:32 * t + 32], T["ID%d" % t][0:16, 0:2], [("ID%d" % t, 0, 2)], [])
-
-        if final:
-            number0()
-        pick(pk, 0, tk, 0, TW, "OF%d" % t, 0, 3)
+    def move(t):
+        pk = "PK%d" % t
         for b in range(3):
             mm(b, "E25Q", 128 * b, pk, 0)
         mm(3, "E25Q", 384, pk, 16, True, False)
         mm(3, "E25Q", 384, pk, 0, False, True)
-        ts(("TT", 1, 2), h1, 0.5, AL.is_lt, fl[3], AL.mult)
-        ts(("OS%d" % t, 0, 4), ("BQ", 0, 4), ("TT", 1, 2), AL.add)
-        w, o, h = ("WN", 0, 128), ("OS%d" % t, 0, 4), ("HC", 0, 64)
-        op("s", lambda q, w=w, o=o, h=h: q.activation(view(h), view(w).indirect(view(o)), AF.Copy), [w, o], [h])
+        mm(7, "WQ", 0, pk, 0)
         for f, b in (("h", 0), ("h", 1), ("n", 0), ("h", 2), ("n", 1), ("n", 2), ("n", 3)):
             c, h = 16 * b, ("PS", 512 * b, 512 * b + 16)
             if f == "h":
                 act(("SS", c, c + 16), ("PS", 512 * b + 16, 512 * b + 32), AF.Copy)
                 tt(("HB", c, c + 16), h, ("SS", c, c + 16), AL.add)
             else:
-                tt(("NEW", b, 64, 4), h if b == 3 else ("HB", c, c + 16), ("HC", c, c + 16), AL.add)
-        qz(hn, CO, 128, "NEW")
-        if not final:
-            for k in "cs":
-                spread(t + 1, k, [efar, enear], hand[k])
-            pick("CA%d" % (t + 1), G * rank, hn, 0, 64 + G, "LC", 0, 1)
-            for b in range(4):
-                act(("WN", 64 + 16 * b, 80 + 16 * b), ("NEW", b, 64, 4), AF.Copy)
-        if t == 0:
-            qz("WQ", 0, 128, "WT")
-        if not final:
-            qz("PK%d" % (t + 1), 0, 144, "ZT")
-            qz("HW%d" % (t + 2), 0, 128, "ZT")
-        mm(6, "WQ", 0, pk, 0)
-        if final:
-            number1()
-            store_ids()
-        for i in range(2):
-            act(("YO", 32 * t + i, 32 * t + 32, 2), ("PS", 3072 + 32 * i, 3072 + 32 * i + 16), AF.Copy)
-        if final:
-            i = (hn + "c", CO, CO + G)
-            dma("y", T.oc[:, 0:4 * G], view(i).bitcast(dt.uint8), [i], [])
+                tt(("NEW", e0 + b, e0 + 64, 4), h if b == 3 else ("HB", c, c + 16), ("HC", c, c + 16), AL.add)
+        qz("CM%d" % (t + 1), q0, 128, "NEW")
+
+    def winner(b, n, a):
+        r = 136 * b
+        scan(("RB", r + 1, r + 1 + n), ("PS", 512 * b, 512 * b + n), ("NEG", 0, n), -1e29, AL.max, AL.max)
+        act(("J", 40 * b, 40 * b + 33), ("RB", r + a, r + a + 33), AF.Sign, bias=("RB", r + n, r + n + 1), scale=-1.0, acc=("WL", b, b + 1))
+
+    def admit(t):
+        tk, ix = "TK%d" % t, ("IX", 0, NB)
+        both = (1 - me, me)
+        for o in both:
+            w, f, v = ("TH", 40 * o, 40 * o + 40), ("HV", TOK * o, TOK * o + TOK), ("VAL", 0, TOK)
+            op("v", lambda e, w=w, f=f, v=v: e.tensor_tensor(view(f), view(w).indirect(view(ix)), view(v), AL.mult), [w, ix, v], [f])
+            w, f, a = ("TO", 40 * o, 40 * o + 40), ("OG", 104 * o + 1, 104 * o + 1 + TOK), ("TT", o, o + 1)
+            op("s", lambda e, w=w, f=f, a=a: e.activation(view(f), view(w).indirect(view(ix)), AF.Identity, accum_out=view(a)), [w, ix], [f, a])
+        for o in both:
+            scan(("CAP", TOK * o, TOK * o + TOK), ("NEG", 0, TOK), ("OG", 104 * o, 104 * o + TOK), ("TT", o, o + 1), AL.max, AL.subtract)
+        for o in both:
+            scan(("SB", 32 + 8 * o, 32 * 97, 32), ("HV", TOK * o, TOK * o + TOK), ("CAP", TOK * o, TOK * o + TOK), 0.0, AL.min, AL.max)
+        for o in both:
+            scan(("SB", 48 + 8 * o, 32 * 97, 32), ("HV", TOK * o, TOK * o + TOK), ("SB", 8 * o, 32 * TOK, 32), 0.0, AL.min, AL.max)
+        turn(("Y1", 0, 32), ("SB", 32 * TOK, 32 * TOK + 32))
+        take("v", ("Y2", 0, 64), ("Y1", 0, 32), ("DL", 0, 4))
+        turn(("RR", 0, 64), ("Y2", 0, 64))
+        for u in range(2):
+            cp(("RR", 64, 128, 8, 64 * u, 64 * u + 64), ("RR", 0, 64, 8, 64 - 64 * u, 128 - 64 * u))
+        for u in (1, 3, 0, 2):
+            cp(("RR", 128, 256, 8, 32 * u, 32 * u + 32), ("RR", 0, 128, 8, 32 * (u ^ 1), 32 * (u ^ 1) + 32))
+        nm = {1 - me: "NM%d" % t, me: "NO%d" % t}
+        for o in both:
+            scan((nm[o], 2, 34, 2), ("RR", 8 * o, 256, 16), ("ZT", 0, 16), 0.0, AL.min, AL.min)
+        for o in both:
+            scan((nm[o], 3, 35, 2), ("RR", 8 * o, 256, 16), (nm[o], 0, 32, 2), 0.0, AL.min, AL.max)
+        send([(eall, "aL%d" % t, (nm[1 - me], 32, 34), [(T.cores[mate], ("LN%d" % t, 0, 2))])])
+        of = "OF%d" % t
+        for i, o in enumerate(both):
+            ts((of, 2 * i, 2 * i + 1), (nm[o], 32, 33), float(Z), AL.add)
+            ts(("KK", i, i + 1), (nm[o], 33, 34), -0.5, AL.is_gt, (nm[o], 32, 33), AL.mult)
+        for i, o in enumerate(both):
+            ts((of, 2 * i + 1, 2 * i + 2), ("KK", i, i + 1), (nm[o], 33, 34), AL.add, float(Z), AL.add)
+        pick("PM%d" % t, 0, tk, 0, Z + 128, of, 0, 2)
+        for k in "cs":
+            send([(eall, "aK%d" % t, ("PM%d%s" % (t, k), 0, 32), [(T.cores[mate], ("PK%d%s" % (t, k), 0, 32))])])
+        pick("PK%d" % t, 0, tk, 0, Z + 128, of, 2, 4)
+
+    late = []
+    for t in range(R):
+        tk, final = "TK%d" % t, t + 1 == R
+        if t % 2 == me:
+            n = ("NO%d" % t, 32, 34)
+            if t == 0:
+                for b in range(NB):
+                    pickc("RP", 128 * b, tk, 0, Z + 128, "RL", 8 * b, 8 * b + 8)
+                for b in range(NB):
+                    picks("sv"[b % 2], "RP", 128 * b, tk, 0, Z + 128, "RL", 8 * b, 8 * b + 8)
+                for b in range(NB):
+                    mm(b, "RP", 128 * b, "CA", 0)
+                for b in range(NB):
+                    winner(b, 128, G * pair[0])
+                cp(("IX", 0, NB), ("WL", 0, NB))
+            else:
+                m = ("MX%d" % t, 0, NB)
+                for b in range(NB):
+                    mm(b, "RP", 128 * b, "CM%d" % t, CA_)
+                for b in range(NB):
+                    i, o = ("PS", 512 * b, 512 * b + 2 * G), ("MX%d" % t, b, b + 1)
+                    op("v", lambda v, i=i, o=o: v.tensor_reduce(view(o), view(i), AX, AL.max), [i], [o])
+                sc = _scorers(t, T, topo)
+
+                def slot(s, d):
+                    i = [r for r in sc if r != d].index(s)
+                    return ("MR%d" % t, 8 * i, 8 * i + NB)
+
+                send([(efar, "aM%d" % t, m, [(T.cores[r], slot(rank, r)) for r in _far(rank, t, T, topo)])])
+                for b in range(NB):
+                    winner(b, 2 * G, 0)
+                old(t)
+                for f in late:
+                    f()
+                late = []
+                low, high = [r for r in sc if r < rank], [r for r in sc if r > rank]
+                two, one = (low[:2], (low + high)[2]) if len(low) >= 2 else (high[-2:], (low + high)[0])
+                c = [("CP", 8 * i, 8 * i + NB) for i in range(5)]
+                tt(c[0], slot(two[0], rank), slot(two[1], rank), AL.max)
+                tt(c[1], m, slot(one, rank), AL.is_gt if one < rank else AL.is_ge)
+                tt(c[2], m, c[0], AL.is_gt if two[0] < rank else AL.is_ge)
+                tt(c[3], c[1], ("WL", 0, NB), AL.mult)
+                tt(c[4], c[2], c[3], AL.mult)
+                cp(("IX", 0, NB), c[4])
+            admit(t)
+            flags(n)
+            move(t)
+            if not final:
+                for k in "cs":
+                    x = ("CM%d%s" % (t + 1, k), co, co + G)
+                    send([(eall, "aN%d" % (t + 1), x, [(T.cores[mate], x)])])
+            numbers(t, n)
+            results(t, "s" if final else "y")
         else:
-            number0()
-            number1()
-            wait("y", ("aC%d" % (t + 1), camec))
-            store_ids()
-        dma("s" if final else "y", T.y[:, 32 * t:32 * t + 32], T.YO[:, 32 * t:32 * t + 32], [("YO", 32 * t, 32 * t + 32)], [])
-        if final:
-            for k in range(4):
-                dma("ys"[k % 2], T.osc[4 * k:4 * k + 4, 0:G], T[hn + "s"][32 * k:32 * k + 4, CO:CO + G], [(hn + "s", CO, CO + G)], [])
+            n = ("LN%d" % t, 0, 2)
+            if t > 0:
+                blank(t)
+                old(t)
+            if not final:
+                blank(t + 1)
+                qz("TK%d" % (t + 1), 128 * rank, 128, "X12", 4 * TOK * t)
+                pick("RP", 0, "TK%d" % (t + 1), 0, Z + 128, "RL", 0, 8 * NB)
+            flags(n)
+            if final:
+                numbers(t, n)
+            move(t)
+            if final:
+                results(t, "s")
+            else:
+                late = [lambda t=t, n=n: numbers(t, n), lambda t=t: results(t, "y")]
+    hn = "CM%d" % R
+    i = (hn + "c", co, co + G)
+    dma("y", T.oc[:, 0:4 * G], view(i).bitcast(dt.uint8), [i], [])
+    for k in range(4):
+        dma("ys"[k % 2], T.osc[4 * k:4 * k + 4, 0:G], T[hn + "s"][32 * k:32 * k + 4, co:co + G], [(hn + "s", co, co + G)], [])
 
     for q in cnt:
         wait("g", (done[q], cnt[q]))
     for i in range(nd[0]):
         wait("g", ("d%d" % i, 16))
+    for tok in outer:
+        wait("g", tok)
     g.wait_ge(T.sem.sent, sent[0])

@@ -9,7 +9,7 @@ CA_ = 128
 
 F32, BF, I32, U16, COD, PLN = "float32", "bfloat16", "int32", "uint16", "float8_e4m3fn_x4", "uint8"
 SCRATCH = {"PS": ("psum", [128, 4096], F32)}
-SEMAPHORES = ["vd", "sd", "pd", "gd", "sent", "aC", "hc0", "hs0", "hc1", "hs1"]
+SEMAPHORES = ["vd", "sd", "pd", "gd", "sent", "aC", "gc", "gs", "hc", "hs"]
 
 
 def _buf(name, n, dtype):
@@ -21,26 +21,25 @@ def _mx(name, n):
     _buf(name + "s", n, PLN)
 
 
-for _n, _w in (("CBT", 512), ("X0", 512), ("X12", 896), ("WT", 512), ("ZT", 512), ("E25", 2048), ("NEW", 512), ("J", 40 * NB)):
+for _n, _w in (("CBT", 512), ("X0", 512), ("X12", 896), ("WT", 512), ("ZT", 512), ("E25", 2048), ("NEW", 512), ("J", 40 * NB),
+               ("NGB", TOK), ("OG", 208), ("CAP", 2 * TOK)):
     _buf(_n, _w, BF)
-for _n, _w in (("NEG", 128), ("DV", 128), ("QC", 1), ("PF", 1), ("VC", 1), ("WI", 40), ("TH", 80), ("TO", 80), ("VAL", 96), ("RB", 136 * NB),
-               ("WL", 8), ("CP", 40), ("HV", 192), ("OG", 208), ("TT", 2), ("CAP", 192), ("SB", 32 * 97), ("Y1", 32), ("Y2", 64), ("RR", 256),
-               ("KK", 2), ("FF", 2), ("IB", 4), ("SS", 64), ("HB", 64), ("WN", 256), ("HC", 64), ("BQ", 4), ("YO", 96), ("YS", 144)):
+for _n, _w in (("NEG", 128), ("DV", 128), ("QC", 1), ("PF", 1), ("VC", 1), ("SG", 1), ("WI", 120), ("TH", 40), ("TO", 80), ("VAL", TOK),
+               ("RB", 136 * NB), ("WL", 4 * NB), ("CP", 4 * NB), ("PR", 4 * NB), ("HV", TOK), ("TT", 2), ("SB", 32 * 97), ("Y1", 32), ("Y2", 64),
+               ("RR", 256), ("KK", 2), ("FF", 2), ("SS", 64), ("HB", 64), ("WN", 256), ("HC", 64), ("BQ", 4), ("YO", 96), ("YS", 144),
+               ("IDT", Z + 8), ("ZC", G), ("ID", 96)):
     _buf(_n, _w, F32)
-for _n, _w in (("QI", 1), ("QJ", 1), ("RI", 48), ("IA", 4)):
+for _n, _w in (("QI", 1), ("QJ", 1), ("RI", 48)):
     _buf(_n, _w, I32)
-for _n, _w in (("RL", 48), ("LC", 2), ("DL", 4), ("IX", 6), ("OS", 4), ("YL", 2)):
+for _n, _w in (("RL", 48), ("LC", 2), ("DL", 4), ("IX", 6), ("IY", 6), ("OS", 4), ("YL", 2), ("IL", 4)):
     _buf(_n, _w, U16)
 for _n, _w in (("XQ", 192), ("WQ", 128), ("E25Q", 512), ("CA", 128), ("RP", 128 * NB)):
     _mx(_n, _w)
 for _t in range(R):
     _mx("TK%d" % _t, Z + 128)
-    _mx("PM%d" % _t, 32)
-    _mx("PK%d" % _t, 160)
-    _buf("NM%d" % _t, 36, F32)
-    _buf("NO%d" % _t, 36, F32)
+    _mx("PK%d" % _t, 192)
+    _buf("NN%d" % _t, 68, F32)
     _buf("LN%d" % _t, 2, F32)
-    _buf("ID%d" % _t, 2, F32)
     _buf("MX%d" % _t, 8, F32)
     _buf("MR%d" % _t, 24, F32)
     _buf("OF%d" % _t, 4, U16)
@@ -89,19 +88,23 @@ def _hand_on(g, core, rank, T, topo, k):
     pair = _pair(rank, T, topo)
     n = [0]
 
-    def on(t, sem, src, dst):
-        sets = [(es, _far(rank, t, T, topo))] + ([(en, [pair[t % 2]])] if pair[t % 2] != rank else [])
+    def on(sets, sem, src, dst):
         g.remote_dma_fused([RemoteDMATransfer(dst_ids=[_dst(T.cores[r], topo) for r in rs], dma_engine_mask=_bits(e), remote_sem=T.sem[sem],
                                               srcs=[byt(src)], dsts=[byt(dst)] * len(rs)) for e, rs in sets], local_sem=T.sem.sent)
         n[0] += sum(len(e) for e, _ in sets)
 
+    def sets(t):
+        return [(es, _far(rank, t, T, topo))] + ([(en, [pair[t % 2]])] if pair[t % 2] != rank else [])
+
     o = CA_ + G * pair.index(rank)
-    g.wait_ge(T.sem["h%s0" % k], came)
-    on(0, "aC", T["CM0" + k][:, o:o + G], T["CA" + k][:, G * rank:G * rank + G])
-    g.wait_ge(T.sem.sent, n[0])
-    g.wait_ge(T.sem["h%s1" % k], came)
+    g.wait_ge(T.sem["g" + k], came)
+    for one in sets(0):
+        on([one], "aC", T["CM0" + k][:, o:o + G], T["CA" + k][:, G * rank:G * rank + G])
+    g.wait_ge(T.sem["h" + k], came)
     for t in range(1, R):
-        on(t, "aT%s%d" % (k, t), T["XQ" + k][:, TOK * (t - 1):TOK * t], T["TK%d%s" % (t, k)][:, 128 * rank:128 * rank + TOK])
+        if t > 1:
+            g.wait_ge(T.sem.sent, n[0])
+        on(sets(t), "aT%s%d" % (k, t), T["XQ" + k][:, TOK * (t - 1):TOK * t], T["TK%d%s" % (t, k)][:, 128 * rank:128 * rank + TOK])
     g.wait_ge(T.sem.sent, n[0])
 
 
@@ -259,6 +262,7 @@ def rank_program(g, core, T, topo):
     efar, eall = topo.engines(core, other), topo.engines(core, T.cores[mate])
     enear = _near_engines(core, T.cores[mate], other, topo)
     hand = {"c": _helper_of(core, T, topo, 0), "s": _helper_of(core, T, topo, 1)}
+    share = len(eall) // NR
     sent = [0]
 
     def send(transfers):
@@ -273,86 +277,106 @@ def rank_program(g, core, T, topo):
         before("g", rd, [])
         g.remote_dma_fused(tr, local_sem=T.sem.sent)
 
-    dma("y", T.CBT[:, e0:e0 + 4 * G], T.cb[:], [], [("CBT", e0, e0 + 4 * G)])
+    def tokens(t, k, r):
+        return ("TK%d%s" % (t, k), 128 * r, 128 * r + TOK)
+
     dma("s", T.X0[:, 0:4 * TOK], T.x[:, 0:4 * TOK], [], [("X0", 0, 4 * TOK)])
+    dma("y", T.CBT[:, e0:e0 + 4 * G], T.cb[:], [], [("CBT", e0, e0 + 4 * G)])
     dma("y", T.X12[:, 0:8 * TOK], T.x[:, 4 * TOK:12 * TOK], [], [("X12", 0, 8 * TOK)])
     dma("s", T.WT[:], T.w[:], [], [("WT", 0, 512)])
     iota(("DV", 0, 128), [[1, 128]], 0, -1)
     iota(("QI", 0, 1), [[0, 1]], 0, 1)
     iota(("RI", 0, 48), [[-G, NB], [128, NR]], TOK - 1, 0)
     rest = (0, e0) if me == 0 else (4 * G, 512)
-    fill(("CBT",) + rest, 0.0)
+    dv, qc = ("DV", 0, 128), ("QC", 0, 1)
     fill(("X0", 4 * TOK, 512), 0.0)
+    fill(("CBT",) + rest, 0.0)
     fill(("ZT", 0, 512), 0.0)
     fill(("X12", 8 * TOK, 896), 0.0)
-    qz("CM0", q0, 128, "CBT")
     qz("TK0", 128 * rank, 128, "X0")
+    qz("CM0", q0, 128, "CBT")
+
+    def first(k):
+        x = tokens(0, k, rank)
+        send([(efar, "aT%s0" % k, x, [(T.cores[r], x) for r in _far(rank, 0, T, topo)])])
+
+    first("c")
     for k in "cs":
         x = ("CM0" + k, co, co + G)
-        send([(enear, "h%s0" % k, x, [(hand[k], x)])])
-    for k in "cs":
-        x = ("TK0" + k, 128 * rank, 128 * rank + TOK)
-        send([(efar, "aT%s0" % k, x, [(T.cores[r], x) for r in _far(rank, 0, T, topo)])] +
-             ([(enear, "aT%s0" % k, x, [(T.cores[mate], x)])] if me == 1 else []))
-    qz("XQ", 0, 2 * TOK, "X12")
-    for k in "cs":
-        x = ("XQ" + k, 0, 2 * TOK)
-        send([(enear, "h%s1" % k, x, [(hand[k], x)])])
+        send([(enear, "g" + k, x, [(hand[k], x)])])
+    first("s")
+    if me == 1:
+        for k in "cs":
+            x = tokens(0, k, rank)
+            send([(enear, "aT%s0" % k, x, [(T.cores[mate], x)])])
     came = len(efar) * (NR - 2) + len(enear)
     for t in range(R):
         if t % 2 == me:
             for k in "cs":
-                ext("aT%s%d" % (k, t), came, [("TK%d%s" % (t, k), 128 * r, 128 * r + TOK) for r in peers])
+                ext("aT%s%d" % (k, t), came, [tokens(t, k, r) for r in peers])
             if t == 0:
                 ext("aC", 2 * came, [("CA" + k, G * r, G * r + G) for k in "cs" for r in peers])
             else:
                 ext("aM%d" % t, 3 * len(efar), [("MR%d" % t, 8 * i, 8 * i + NB) for i in range(3)])
                 o = CA_ + G * (1 - me)
                 ext("aN%d" % t, 2 * len(eall), [("CM%d%s" % (t, k), o, o + G) for k in "cs"])
-        else:
+        elif t + 1 < R:
             ext("aL%d" % t, len(eall), [("LN%d" % t, 0, 2)])
             ext("aK%d" % t, 2 * len(eall), [("PK%d%s" % (t, k), 0, 32) for k in "cs"])
+        else:
+            ext("aL%d" % t, len(eall), [("IY", 0, NB)])
+            for k in "cs":
+                ext("aT%s%d" % (k, t), share * len(peers), [tokens(t, k, r) for r in peers])
 
-    dv, qc = ("DV", 0, 128), ("QC", 0, 1)
+    sign = (1.0, -1.0)
     for b in range(4):
         act(("E25", 512 * b, 512 * b + 512), ("ZT", 0, 512), AF.Copy)
     act(("NEG", 0, 128), ("ZT", 0, 128), AF.Identity, bias=-1e29)
+    act(("NGB", 0, TOK), ("ZT", 0, TOK), AF.Identity, bias=-1e29)
     act(("WN", 128, 256), ("ZT", 0, 128), AF.Copy)
     act(("YS", 16, 144), ("ZT", 0, 128), AF.Copy)
     act(("NEW",) + rest, ("ZT",) + rest, AF.Copy)
+    for x in (("SB", 0, 32), ("SB", 32 * TOK, 32 * TOK + 32), ("WL", 0, 4 * NB), ("CP", 0, 4 * NB), ("TO", 0, 80)):
+        act(x, ("ZT", 0, x[2] - x[1]), AF.Copy)
     ts(("QJ", 0, 1), ("QI", 0, 1), 15, AL.bitwise_and)
     cp(("PF", 0, 1), ("QI", 0, 1))
     cp(qc, ("QJ", 0, 1))
-    fill(("TO", 0, 80), 0.0)
+    fill(("RB", 0, 136 * NB, 136), -1e29)
     ts(("WI", 0, 40), ("DV", 0, 40), ("PF", 0, 1), AL.add)
     ts(("RL", 0, 48), ("RI", 0, 48), qc, AL.subtract)
     ts(("LC", 0, 1), qc, 0.0, AL.add)
     ts(("VC", 0, 1), qc, -8.0, AL.mult, float(TOK - 1 - Z), AL.add)
+    ts(("SG", 0, 1), qc, 7.5, AL.is_ge, -2.0, AL.mult)
     for o in range(2):
-        fill(("TO", 40 * o + 1 + G * o, 40 * o + 1 + G * o + G), BIG)
-        ts(("TH", 40 * o, 40 * o + 40), ("WI", 0, 40), qc, AL.subtract, float(1 + G * o), AL.is_equal)
+        ts(("WI", 40 + 40 * o, 80 + 40 * o), ("WI", 0, 40), qc, AL.subtract, float(1 + G * o), AL.is_equal)
         ts(("DL", 2 * o, 2 * o + 2), ("ZT", 0, 2), qc, AL.add, float(G * o), AL.add)
+        fill(("OG", 104 * o, 104 * o + 1), sign[o] * (CAPP + 1) * BIG)
     ts(("VC", 0, 1), ("PF", 0, 1), 7.0, AL.mult, ("VC", 0, 1), AL.add)
+    ts(("SG", 0, 1), ("SG", 0, 1), 1.0, AL.add)
+    tt(("TH", 0, 40), ("WI", 40, 80), ("WI", 80, 120), AL.subtract)
+    ts(("VAL", 0, TOK), ("DV", 0, TOK), -1.0, AL.mult, ("VC", 0, 1), AL.add)
+    qz("XQ", 0, 2 * TOK, "X12")
+    for k in "cs":
+        x = ("XQ" + k, 0, 2 * TOK)
+        send([(enear, "h" + k, x, [(hand[k], x)])])
+    iota(("IDT", 0, Z), [[TOK, NR], [1, 128]], 0, 0)
+    for t in range(R):
+        if t % 2 == me or t + 1 == R:
+            fill(("NN%d" % t, 0, 4), float(Z))
+    fill(("ZC", 0, G), float(Z))
     if me == 0:
         pick("CA", G * rank, "CM0", CA_, CA_ + G, "LC", 0, 1)
-    fill(("OG", 0, 208, 104), (CAPP + 1) * BIG)
-    fill(("RB", 0, 136 * NB, 136), -1e29)
-    ts(("VAL", 0, TOK), ("DV", 0, TOK), -1.0, AL.mult, ("VC", 0, 1), AL.add)
-    fill(("SB", 0, 32), 0.0)
-    fill(("SB", 32 * TOK, 32 * TOK + 32), 0.0)
-    for t in range(R):
-        if t % 2 == me:
-            fill(("NM%d" % t, 0, 1), 0.0)
-            fill(("NO%d" % t, 0, 1), 0.0)
     for b in range(4):
         ts(("E25", 512 * b + b, 512 * b + 512, 4), dv, 0.0, AL.is_equal, 0.25, AL.mult)
         act(("BQ", b, b + 1), qc, AF.Identity, bias=float(32 * b + G * me))
+    for o in range(2):
+        fill(("TO", 40 * o + 1 + G * o, 40 * o + 1 + G * o + G), sign[o] * BIG)
 
     def blank(t):
         lands = t > 0 and t % 2 == me
         qz("CM%d" % t, (CA_ + 2 * G if lands else CA_ + G) if me == 0 else (0 if lands else G), 128, "ZT")
-        qz("PK%d" % t, 32, 128, "ZT")
-        if t % 2 == me:
+        qz("PK%d" % t, 64 if t % 2 == me and t + 1 < R else 32, 128, "ZT")
+        if t % 2 == me or t + 1 == R:
             qz("TK%d" % t, Z, 128, "ZT")
 
     def old(t):
@@ -366,22 +390,24 @@ def rank_program(g, core, T, topo):
     blank(0)
     qz("E25Q", 0, 512, "E25")
     qz("WQ", 0, 128, "WT")
+    fill(("IDT", Z, Z + 1), -1.0)
     old(0)
 
-    def flags(n):
-        ts(("FF", 0, 2), n, -0.5, AL.is_gt, 128.0, AL.mult)
-        ts(("OS", 0, 4), ("BQ", 0, 4), ("FF", 0, 1), AL.add)
-        take("s", ("HC", 0, 64), ("WN", 0, 256), ("OS", 0, 4))
+    def none(n):
+        ts(("FF", 0, 2), n, Z - 0.5, AL.is_ge, 128.0, AL.mult)
 
-    def numbers(t, n):
-        ts(("IA", 0, 2), n, float(Z), AL.add)
-        ts(("YL", 0, 1), qc, ("FF", 1, 2), AL.add)
-        ts(("IA", 2, 4), ("IA", 0, 2), 7, AL.arith_shift_right)
-        ts(("IB", 0, 2), ("IA", 2, 4), float(TOK - 128), AL.mult, float(Z), AL.add)
-        tt(("IB", 2, 4), ("IB", 0, 2), n, AL.add)
+    def flags(n, now):
+        ts(("OS", 0, 4), ("BQ", 0, 4), ("FF", 0, 1), AL.add)
+        if now:
+            ts(("YL", 0, 1), qc, ("FF", 1, 2), AL.add)
+        take("v", ("HC", 0, 64), ("WN", 0, 256), ("OS", 0, 4))
+        if now:
+            cp(("IL", 0, 4, 2), n)
+
+    def numbers(t):
         for i in range(2):
-            ts(("ID%d" % t, i, i + 1), ("FF", i, i + 1), -(NR * TOK + 1) / 128.0, AL.mult, ("IB", 2 + i, 3 + i), AL.add)
-        dma("y", T.ids[:, 32 * t:32 * t + 32], T["ID%d" % t][0:16, 0:2], [("ID%d" % t, 0, 2)], [])
+            take("s", ("ID", 32 * t + i, 32 * t + 32, 2), ("IDT", 0, Z + 1), ("IL", 2 * i, 2 * i + 1))
+        dma("y", T.ids[:, 32 * t:32 * t + 32], T.ID[0:1, 32 * t:32 * t + 32], [("ID", 32 * t, 32 * t + 32)], [])
 
     def results(t, q):
         act(("YS", 0, G), ("PS", 3584 + G, 3584 + 2 * G), AF.Copy)
@@ -389,80 +415,96 @@ def rank_program(g, core, T, topo):
         take("s", ("YO", 32 * t + 1, 32 * t + 32, 2), ("YS", 0, 144), ("YL", 0, 1))
         dma(q, T.y[:, 32 * t:32 * t + 32], T.YO[:, 32 * t:32 * t + 32], [("YO", 32 * t, 32 * t + 32)], [])
 
+    def stores(t):
+        wait("y", (done["s"], cnt["s"]))
+        numbers(t)
+        results(t, "y")
+
     def move(t):
         pk = "PK%d" % t
-        for b in range(3):
+        for b in range(2):
             mm(b, "E25Q", 128 * b, pk, 0)
-        mm(3, "E25Q", 384, pk, 16, True, False)
-        mm(3, "E25Q", 384, pk, 0, False, True)
+        for b in range(2, 4):
+            mm(b, "E25Q", 128 * b, pk, 16, True, False)
+            mm(b, "E25Q", 128 * b, pk, 0, False, True)
         mm(7, "WQ", 0, pk, 0)
-        for f, b in (("h", 0), ("h", 1), ("n", 0), ("h", 2), ("n", 1), ("n", 2), ("n", 3)):
+        for f, b in (("h", 0), ("h", 1), ("n", 0), ("n", 1), ("n", 2), ("n", 3)):
             c, h = 16 * b, ("PS", 512 * b, 512 * b + 16)
             if f == "h":
                 act(("SS", c, c + 16), ("PS", 512 * b + 16, 512 * b + 32), AF.Copy)
                 tt(("HB", c, c + 16), h, ("SS", c, c + 16), AL.add)
+                if b == 1 and t + 1 == R:
+                    numbers(t)
             else:
-                tt(("NEW", e0 + b, e0 + 64, 4), h if b == 3 else ("HB", c, c + 16), ("HC", c, c + 16), AL.add)
+                tt(("NEW", e0 + b, e0 + 64, 4), h if b >= 2 else ("HB", c, c + 16), ("HC", c, c + 16), AL.add)
         qz("CM%d" % (t + 1), q0, 128, "NEW")
 
     def winner(b, n, a):
         r = 136 * b
         scan(("RB", r + 1, r + 1 + n), ("PS", 512 * b, 512 * b + n), ("NEG", 0, n), -1e29, AL.max, AL.max)
-        act(("J", 40 * b, 40 * b + 33), ("RB", r + a, r + a + 33), AF.Sign, bias=("RB", r + n, r + n + 1), scale=-1.0, acc=("WL", b, b + 1))
+        act(("J", 40 * b, 40 * b + 33), ("RB", r + a, r + a + 33), AF.Sign, bias=("RB", r + n, r + n + 1), scale=-1.0, acc=("WL", 4 * b, 4 * b + 1))
 
-    def admit(t):
-        tk, ix = "TK%d" % t, ("IX", 0, NB)
-        both = (1 - me, me)
+    def admit(t, both, ix):
+        tk, hv = "TK%d" % t, ("HV", 0, TOK)
+        best = {0: (AL.min, AL.max), 1: (AL.max, AL.min)}
+        w, v = ("TH", 0, 40), ("VAL", 0, TOK)
+        op("v", lambda e: e.tensor_tensor(view(hv), view(w).indirect(view(ix)), view(v), AL.mult), [w, ix, v], [hv])
         for o in both:
-            w, f, v = ("TH", 40 * o, 40 * o + 40), ("HV", TOK * o, TOK * o + TOK), ("VAL", 0, TOK)
-            op("v", lambda e, w=w, f=f, v=v: e.tensor_tensor(view(f), view(w).indirect(view(ix)), view(v), AL.mult), [w, ix, v], [f])
-            w, f, a = ("TO", 40 * o, 40 * o + 40), ("OG", 104 * o + 1, 104 * o + 1 + TOK), ("TT", o, o + 1)
-            op("s", lambda e, w=w, f=f, a=a: e.activation(view(f), view(w).indirect(view(ix)), AF.Identity, accum_out=view(a)), [w, ix], [f, a])
+            w2, f, a = ("TO", 40 * o, 40 * o + 40), ("OG", 104 * o + 1, 104 * o + 1 + TOK), ("TT", o, o + 1)
+            op("s", lambda e, w2=w2, f=f, a=a: e.activation(view(f), view(w2).indirect(view(ix)), AF.Identity, accum_out=view(a)), [w2, ix], [f, a])
+        steps = []
         for o in both:
-            scan(("CAP", TOK * o, TOK * o + TOK), ("NEG", 0, TOK), ("OG", 104 * o, 104 * o + TOK), ("TT", o, o + 1), AL.max, AL.subtract)
-        for o in both:
-            scan(("SB", 32 + 8 * o, 32 * 97, 32), ("HV", TOK * o, TOK * o + TOK), ("CAP", TOK * o, TOK * o + TOK), 0.0, AL.min, AL.max)
-        for o in both:
-            scan(("SB", 48 + 8 * o, 32 * 97, 32), ("HV", TOK * o, TOK * o + TOK), ("SB", 8 * o, 32 * TOK, 32), 0.0, AL.min, AL.max)
+            cap = ("CAP", TOK * o, TOK * o + TOK)
+            steps.append([
+                lambda o=o, cap=cap: scan(cap, ("NGB", 0, TOK), ("OG", 104 * o, 104 * o + TOK), ("TT", o, o + 1), AL.max, AL.subtract),
+                lambda o=o, cap=cap: scan(("SB", 32 + 8 * o, 32 * 97, 32), hv, cap, 0.0, best[o][0], best[o][1]),
+                lambda o=o: scan(("SB", 48 + 8 * o, 32 * 97, 32), hv, ("SB", 8 * o, 32 * TOK, 32), 0.0, best[o][0], best[o][1])])
+        for i, j in ((0, 0), (0, 1), (1, 0), (0, 2), (1, 1), (1, 2)):
+            if i < len(both):
+                steps[i][j]()
         turn(("Y1", 0, 32), ("SB", 32 * TOK, 32 * TOK + 32))
-        take("v", ("Y2", 0, 64), ("Y1", 0, 32), ("DL", 0, 4))
-        turn(("RR", 0, 64), ("Y2", 0, 64))
+        y1, y2, dl, sg = ("Y1", 0, 32), ("Y2", 0, 64), ("DL", 0, 4), ("SG", 0, 1)
+        op("v", lambda e: e.tensor_scalar(view(y2), view(y1).indirect(view(dl)), view(sg), float(Z), AL.mult, AL.add), [y1, dl, sg], [y2])
+        turn(("RR", 0, 64), y2)
+        shift = {"v": cp, "s": lambda o, i: act(o, i, AF.Copy)}
         for u in range(2):
-            cp(("RR", 64, 128, 8, 64 * u, 64 * u + 64), ("RR", 0, 64, 8, 64 - 64 * u, 128 - 64 * u))
-        for u in (1, 3, 0, 2):
-            cp(("RR", 128, 256, 8, 32 * u, 32 * u + 32), ("RR", 0, 128, 8, 32 * (u ^ 1), 32 * (u ^ 1) + 32))
-        nm = {1 - me: "NM%d" % t, me: "NO%d" % t}
+            shift["vs"[u]](("RR", 64, 128, 8, 64 * u, 64 * u + 64), ("RR", 0, 64, 8, 64 - 64 * u, 128 - 64 * u))
+        for u in range(4):
+            shift["vs"[u // 2]](("RR", 128, 256, 8, 32 * u, 32 * u + 32), ("RR", 0, 128, 8, 32 * (u ^ 1), 32 * (u ^ 1) + 32))
+        nn, of, at = "NN%d" % t, "OF%d" % t, {me: 0, 1 - me: 2}
         for o in both:
-            scan((nm[o], 2, 34, 2), ("RR", 8 * o, 256, 16), ("ZT", 0, 16), 0.0, AL.min, AL.min)
+            scan((nn, 4 + at[o], 68, 4), ("RR", 8 * o, 256, 16), ("ZC", 0, G), float(Z), AL.min, AL.min)
         for o in both:
-            scan((nm[o], 3, 35, 2), ("RR", 8 * o, 256, 16), (nm[o], 0, 32, 2), 0.0, AL.min, AL.max)
-        send([(eall, "aL%d" % t, (nm[1 - me], 32, 34), [(T.cores[mate], ("LN%d" % t, 0, 2))])])
-        of = "OF%d" % t
-        for i, o in enumerate(both):
-            ts((of, 2 * i, 2 * i + 1), (nm[o], 32, 33), float(Z), AL.add)
-            ts(("KK", i, i + 1), (nm[o], 33, 34), -0.5, AL.is_gt, (nm[o], 32, 33), AL.mult)
-        for i, o in enumerate(both):
-            ts((of, 2 * i + 1, 2 * i + 2), ("KK", i, i + 1), (nm[o], 33, 34), AL.add, float(Z), AL.add)
-        pick("PM%d" % t, 0, tk, 0, Z + 128, of, 0, 2)
-        for k in "cs":
-            send([(eall, "aK%d" % t, ("PM%d%s" % (t, k), 0, 32), [(T.cores[mate], ("PK%d%s" % (t, k), 0, 32))])])
-        pick("PK%d" % t, 0, tk, 0, Z + 128, of, 2, 4)
+            scan((nn, 5 + at[o], 68, 4), ("RR", 8 * o, 256, 16), (nn, at[o], 64, 4), float(Z), AL.min, AL.max)
+        if len(both) > 1:
+            send([(eall, "aL%d" % t, (nn, 66, 68), [(T.cores[mate], ("LN%d" % t, 0, 2))])])
+        w3 = 2 * len(both)
+        cp((of, 0, w3, 2), (nn, 64, 64 + w3, 2))
+        ts(("KK", 0, len(both)), (nn, 65, 64 + w3, 2), Z - 0.5, AL.is_ge, -BIG, AL.mult)
+        none((nn, 64, 66))
+        for o in both:
+            c = at[o]
+            ts((of, c + 1, c + 2), ("KK", c // 2, c // 2 + 1), (nn, 65 + c, 66 + c), AL.add, (nn, 64 + c, 65 + c), AL.max)
+        pick("PK%d" % t, 0, tk, 0, Z + 128, of, 0, w3)
+        if len(both) > 1:
+            for k in "cs":
+                send([(eall, "aK%d" % t, ("PK%d%s" % (t, k), 32, 64), [(T.cores[mate], ("PK%d%s" % (t, k), 0, 32))])])
 
     late = []
     for t in range(R):
         tk, final = "TK%d" % t, t + 1 == R
+        ix, n = ("IX", 0, NB), ("NN%d" % t, 64, 66)
         if t % 2 == me:
-            n = ("NO%d" % t, 32, 34)
             if t == 0:
                 for b in range(NB):
                     pickc("RP", 128 * b, tk, 0, Z + 128, "RL", 8 * b, 8 * b + 8)
                 for b in range(NB):
-                    picks("sv"[b % 2], "RP", 128 * b, tk, 0, Z + 128, "RL", 8 * b, 8 * b + 8)
+                    picks("ssvsvs"[b], "RP", 128 * b, tk, 0, Z + 128, "RL", 8 * b, 8 * b + 8)
                 for b in range(NB):
                     mm(b, "RP", 128 * b, "CA", 0)
                 for b in range(NB):
                     winner(b, 128, G * pair[0])
-                cp(("IX", 0, NB), ("WL", 0, NB))
+                cp(ix, ("WL", 0, 4 * NB, 4))
             else:
                 m = ("MX%d" % t, 0, NB)
                 for b in range(NB):
@@ -483,41 +525,49 @@ def rank_program(g, core, T, topo):
                 for f in late:
                     f()
                 late = []
-                low, high = [r for r in sc if r < rank], [r for r in sc if r > rank]
-                two, one = (low[:2], (low + high)[2]) if len(low) >= 2 else (high[-2:], (low + high)[0])
-                c = [("CP", 8 * i, 8 * i + NB) for i in range(5)]
-                tt(c[0], slot(two[0], rank), slot(two[1], rank), AL.max)
-                tt(c[1], m, slot(one, rank), AL.is_gt if one < rank else AL.is_ge)
-                tt(c[2], m, c[0], AL.is_gt if two[0] < rank else AL.is_ge)
-                tt(c[3], c[1], ("WL", 0, NB), AL.mult)
-                tt(c[4], c[2], c[3], AL.mult)
-                cp(("IX", 0, NB), c[4])
-            admit(t)
-            flags(n)
-            move(t)
-            if not final:
-                for k in "cs":
-                    x = ("CM%d%s" % (t + 1, k), co, co + G)
-                    send([(eall, "aN%d" % (t + 1), x, [(T.cores[mate], x)])])
-            numbers(t, n)
-            results(t, "s" if final else "y")
-        else:
-            n = ("LN%d" % t, 0, 2)
-            if t > 0:
-                blank(t)
-                old(t)
-            if not final:
-                blank(t + 1)
-                qz("TK%d" % (t + 1), 128 * rank, 128, "X12", 4 * TOK * t)
-                pick("RP", 0, "TK%d" % (t + 1), 0, Z + 128, "RL", 0, 8 * NB)
-            flags(n)
+                for i, r in enumerate([r for r in sc if r != rank]):
+                    tt(("CP", 1 + i, 4 * NB, 4), m, slot(r, rank), AL.is_gt if r < rank else AL.is_ge)
+                scan(("PR", 0, 4 * NB), ("CP", 0, 4 * NB), ("WL", 0, 4 * NB), 0.0, AL.mult, AL.add)
+                cp(ix, ("PR", 3, 4 * NB, 4))
             if final:
-                numbers(t, n)
+                send([(eall, "aL%d" % t, ix, [(T.cores[mate], ("IY", 0, NB))])])
+            admit(t, (me,) if final else (1 - me, me), ix)
+            flags(n, final)
             move(t)
             if final:
                 results(t, "s")
             else:
-                late = [lambda t=t, n=n: numbers(t, n), lambda t=t: results(t, "y")]
+                for k in "cs":
+                    x = ("CM%d%s" % (t + 1, k), co, co + G)
+                    send([(eall, "aN%d" % (t + 1), x, [(T.cores[mate], x)])])
+                ts(("YL", 0, 1), qc, ("FF", 1, 2), AL.add)
+                cp(("IL", 0, 4, 2), n)
+        elif final:
+            blank(t)
+            old(t)
+            stores(t - 1)
+            admit(t, (me,), ("IY", 0, NB))
+            flags(n, True)
+            move(t)
+            results(t, "s")
+        else:
+            if t > 0:
+                blank(t)
+                old(t)
+                stores(t - 1)
+            blank(t + 1)
+            qz("TK%d" % (t + 1), 128 * rank, 128, "X12", 4 * TOK * t)
+            if t + 2 == R:
+                for k in "cs":
+                    send([(eall[share * i:share * i + share], "aT%s%d" % (k, t + 1), tokens(t + 1, k, r), [(T.cores[mate], tokens(t + 1, k, r))])
+                          for i, r in enumerate([r for r in range(NR) if r != mate])])
+            else:
+                qz("TK%d" % (R - 1), 128 * rank, 128, "X12", 4 * TOK * (R - 2))
+            pick("RP", 0, "TK%d" % (t + 1), 0, Z + 128, "RL", 0, 8 * NB)
+            none(("LN%d" % t, 0, 2))
+            flags(("LN%d" % t, 0, 2), True)
+            move(t)
+            late = [lambda t=t: numbers(t), lambda t=t: results(t, "y")]
     hn = "CM%d" % R
     i = (hn + "c", co, co + G)
     dma("y", T.oc[:, 0:4 * G], view(i).bitcast(dt.uint8), [i], [])

@@ -6,10 +6,11 @@ NB = TOK // G
 Z = 128 * NR
 BIG = 2048.0
 CA_ = 128
+BY = {"c": 3, "s": 2}
 
 F32, BF, I32, U16, COD, PLN = "float32", "bfloat16", "int32", "uint16", "float8_e4m3fn_x4", "uint8"
 SCRATCH = {"PS": ("psum", [128, 4096], F32)}
-SEMAPHORES = ["vd", "sd", "pd", "gd", "sent", "aC", "gc", "gs", "hc", "hs"]
+SEMAPHORES = ["vd", "sd", "pd", "gd", "sent", "aC", "gc", "gs", "hc1", "hs1", "hc2", "hs2"]
 
 
 def _buf(name, n, dtype):
@@ -24,14 +25,14 @@ def _mx(name, n):
 for _n, _w in (("CBT", 512), ("X0", 512), ("X12", 896), ("WT", 512), ("ZT", 512), ("E25", 2048), ("NEW", 512), ("J", 40 * NB),
                ("NGB", TOK), ("OG", 208), ("CAP", 2 * TOK)):
     _buf(_n, _w, BF)
-for _n, _w in (("NEG", 128), ("DV", 128), ("QC", 1), ("PF", 1), ("VC", 1), ("SG", 1), ("WI", 120), ("TH", 40), ("TO", 80), ("VAL", TOK),
-               ("RB", 136 * NB), ("WL", 4 * NB), ("CP", 4 * NB), ("PR", 4 * NB), ("HV", TOK), ("TT", 2), ("SB", 32 * 97), ("Y1", 32), ("Y2", 64),
-               ("RR", 256), ("KK", 2), ("FF", 2), ("SS", 64), ("HB", 64), ("WN", 256), ("HC", 64), ("BQ", 4), ("YO", 96), ("YS", 144),
-               ("IDT", Z + 8), ("ZC", G), ("ID", 96)):
+for _n, _w in (("NEG", 128), ("AB", 128), ("DV", 128), ("QC", 1), ("PF", 1), ("VC", 1), ("WI", 120), ("TO", 80), ("VAL", TOK),
+               ("RB", 136 * NB), ("WL", 4 * NB), ("CP", 4 * NB), ("PR", 4 * NB), ("HV", 2 * TOK), ("JS", 2 * G), ("SU", 2), ("TT", 2),
+               ("SB", 32 * 104), ("Y2", 64), ("KK", 2), ("FF", 2), ("SS", 64), ("HB", 64), ("WN", 256), ("HC", 64), ("BQ", 4),
+               ("YO", 96), ("YS", 144), ("IDT", Z + 8), ("ID", 96)):
     _buf(_n, _w, F32)
 for _n, _w in (("QI", 1), ("QJ", 1), ("RI", 48)):
     _buf(_n, _w, I32)
-for _n, _w in (("RL", 48), ("LC", 2), ("DL", 4), ("IX", 6), ("IY", 6), ("OS", 4), ("YL", 2), ("IL", 4)):
+for _n, _w in (("RL", 48), ("LC", 2), ("IX", 6), ("IY", 6), ("OS", 4), ("YL", 2), ("IL", 4)):
     _buf(_n, _w, U16)
 for _n, _w in (("XQ", 192), ("WQ", 128), ("E25Q", 512), ("CA", 128), ("RP", 128 * NB)):
     _mx(_n, _w)
@@ -43,7 +44,7 @@ for _t in range(R):
     _buf("MX%d" % _t, 8, F32)
     _buf("MR%d" % _t, 24, F32)
     _buf("OF%d" % _t, 4, U16)
-    SEMAPHORES += ["aTc%d" % _t, "aTs%d" % _t, "aL%d" % _t, "aK%d" % _t, "aM%d" % _t, "aN%d" % _t]
+    SEMAPHORES += ["aTc%d" % _t, "aTs%d" % _t, "aL%d" % _t, "aK%d" % _t, "aN%d" % _t] + ["aM%d%d" % (_t, _i) for _i in range(3)]
 for _t in range(R + 1):
     _mx("CM%d" % _t, 288)
 SEMAPHORES += ["d%d" % _i for _i in range(24)]
@@ -98,10 +99,10 @@ def _hand_on(g, core, rank, T, topo, k):
 
     o = CA_ + G * pair.index(rank)
     g.wait_ge(T.sem["g" + k], came)
-    for one in sets(0):
-        on([one], "aC", T["CM0" + k][:, o:o + G], T["CA" + k][:, G * rank:G * rank + G])
-    g.wait_ge(T.sem["h" + k], came)
+    for e, rs in sets(0):
+        on([(e, rs[:BY[k]])], "aC", T["CM0" + k][:, o:o + G], T["CA" + k][:, G * rank:G * rank + G])
     for t in range(1, R):
+        g.wait_ge(T.sem["h%s%d" % (k, t)], came)
         if t > 1:
             g.wait_ge(T.sem.sent, n[0])
         on(sets(t), "aT%s%d" % (k, t), T["XQ" + k][:, TOK * (t - 1):TOK * t], T["TK%d%s" % (t, k)][:, 128 * rank:128 * rank + TOK])
@@ -258,11 +259,12 @@ def rank_program(g, core, T, topo):
             log.setdefault(nm, []).append(("w", cs, (sem, val), "x"))
 
     peers = [r for r in range(NR) if r != rank]
-    other = T.cores[_far(rank, 0, T, topo)[0]]
+    far0 = _far(rank, 0, T, topo)
+    other = T.cores[far0[0]]
     efar, eall = topo.engines(core, other), topo.engines(core, T.cores[mate])
     enear = _near_engines(core, T.cores[mate], other, topo)
     hand = {"c": _helper_of(core, T, topo, 0), "s": _helper_of(core, T, topo, 1)}
-    share = len(eall) // NR
+    share = {"c": (eall, len(eall) // NR), "s": (enear, len(enear) // NR)}
     sent = [0]
 
     def send(transfers):
@@ -298,13 +300,16 @@ def rank_program(g, core, T, topo):
 
     def first(k):
         x = tokens(0, k, rank)
-        send([(efar, "aT%s0" % k, x, [(T.cores[r], x) for r in _far(rank, 0, T, topo)])])
+        send([(efar, "aT%s0" % k, x, [(T.cores[r], x) for r in far0])])
 
     first("c")
     for k in "cs":
         x = ("CM0" + k, co, co + G)
         send([(enear, "g" + k, x, [(hand[k], x)])])
     first("s")
+    for k in "cs":
+        for r in far0[BY[k]:]:
+            send([(efar, "aC", ("CM0" + k, co, co + G), [(T.cores[r], ("CA" + k, G * rank, G * rank + G))])])
     if me == 1:
         for k in "cs":
             x = tokens(0, k, rank)
@@ -317,7 +322,8 @@ def rank_program(g, core, T, topo):
             if t == 0:
                 ext("aC", 2 * came, [("CA" + k, G * r, G * r + G) for k in "cs" for r in peers])
             else:
-                ext("aM%d" % t, 3 * len(efar), [("MR%d" % t, 8 * i, 8 * i + NB) for i in range(3)])
+                for i in range(3):
+                    ext("aM%d%d" % (t, i), len(efar), [("MR%d" % t, 8 * i, 8 * i + NB)])
                 o = CA_ + G * (1 - me)
                 ext("aN%d" % t, 2 * len(eall), [("CM%d%s" % (t, k), o, o + G) for k in "cs"])
         elif t + 1 < R:
@@ -326,51 +332,7 @@ def rank_program(g, core, T, topo):
         else:
             ext("aL%d" % t, len(eall), [("IY", 0, NB)])
             for k in "cs":
-                ext("aT%s%d" % (k, t), share * len(peers), [tokens(t, k, r) for r in peers])
-
-    sign = (1.0, -1.0)
-    for b in range(4):
-        act(("E25", 512 * b, 512 * b + 512), ("ZT", 0, 512), AF.Copy)
-    act(("NEG", 0, 128), ("ZT", 0, 128), AF.Identity, bias=-1e29)
-    act(("NGB", 0, TOK), ("ZT", 0, TOK), AF.Identity, bias=-1e29)
-    act(("WN", 128, 256), ("ZT", 0, 128), AF.Copy)
-    act(("YS", 16, 144), ("ZT", 0, 128), AF.Copy)
-    act(("NEW",) + rest, ("ZT",) + rest, AF.Copy)
-    for x in (("SB", 0, 32), ("SB", 32 * TOK, 32 * TOK + 32), ("WL", 0, 4 * NB), ("CP", 0, 4 * NB), ("TO", 0, 80)):
-        act(x, ("ZT", 0, x[2] - x[1]), AF.Copy)
-    ts(("QJ", 0, 1), ("QI", 0, 1), 15, AL.bitwise_and)
-    cp(("PF", 0, 1), ("QI", 0, 1))
-    cp(qc, ("QJ", 0, 1))
-    fill(("RB", 0, 136 * NB, 136), -1e29)
-    ts(("WI", 0, 40), ("DV", 0, 40), ("PF", 0, 1), AL.add)
-    ts(("RL", 0, 48), ("RI", 0, 48), qc, AL.subtract)
-    ts(("LC", 0, 1), qc, 0.0, AL.add)
-    ts(("VC", 0, 1), qc, -8.0, AL.mult, float(TOK - 1 - Z), AL.add)
-    ts(("SG", 0, 1), qc, 7.5, AL.is_ge, -2.0, AL.mult)
-    for o in range(2):
-        ts(("WI", 40 + 40 * o, 80 + 40 * o), ("WI", 0, 40), qc, AL.subtract, float(1 + G * o), AL.is_equal)
-        ts(("DL", 2 * o, 2 * o + 2), ("ZT", 0, 2), qc, AL.add, float(G * o), AL.add)
-        fill(("OG", 104 * o, 104 * o + 1), sign[o] * (CAPP + 1) * BIG)
-    ts(("VC", 0, 1), ("PF", 0, 1), 7.0, AL.mult, ("VC", 0, 1), AL.add)
-    ts(("SG", 0, 1), ("SG", 0, 1), 1.0, AL.add)
-    tt(("TH", 0, 40), ("WI", 40, 80), ("WI", 80, 120), AL.subtract)
-    ts(("VAL", 0, TOK), ("DV", 0, TOK), -1.0, AL.mult, ("VC", 0, 1), AL.add)
-    qz("XQ", 0, 2 * TOK, "X12")
-    for k in "cs":
-        x = ("XQ" + k, 0, 2 * TOK)
-        send([(enear, "h" + k, x, [(hand[k], x)])])
-    iota(("IDT", 0, Z), [[TOK, NR], [1, 128]], 0, 0)
-    for t in range(R):
-        if t % 2 == me or t + 1 == R:
-            fill(("NN%d" % t, 0, 4), float(Z))
-    fill(("ZC", 0, G), float(Z))
-    if me == 0:
-        pick("CA", G * rank, "CM0", CA_, CA_ + G, "LC", 0, 1)
-    for b in range(4):
-        ts(("E25", 512 * b + b, 512 * b + 512, 4), dv, 0.0, AL.is_equal, 0.25, AL.mult)
-        act(("BQ", b, b + 1), qc, AF.Identity, bias=float(32 * b + G * me))
-    for o in range(2):
-        fill(("TO", 40 * o + 1 + G * o, 40 * o + 1 + G * o + G), sign[o] * BIG)
+                ext("aT%s%d" % (k, t), share[k][1] * len(peers), [tokens(t, k, r) for r in peers])
 
     def blank(t):
         lands = t > 0 and t % 2 == me
@@ -387,54 +349,101 @@ def rank_program(g, core, T, topo):
             c = 128 + 32 * b + G * me
             act(("WN", c, c + G), ("CBT" if t == 0 else "NEW", e0 + b, e0 + 64, 4), AF.Copy)
 
+    def put(x, c):
+        n = len(range(x[1], x[2], x[3] if len(x) > 3 else 1))
+        act(x, ("ZT", 0, n), AF.Identity, bias=float(c))
+
+    act(("AB", 0, 128), dv, AF.Abs)
+    for b in range(4):
+        act(("E25", 512 * b, 512 * b + 512), ("ZT", 0, 512), AF.Copy)
+    for b in range(4):
+        act(("E25", 512 * b + b, 512 * b + 512, 4), ("AB", 0, 128), AF.Relu, bias=0.25, scale=-1.0)
+    ts(("QJ", 0, 1), ("QI", 0, 1), 15, AL.bitwise_and)
+    cp(("PF", 0, 1), ("QI", 0, 1))
+    cp(qc, ("QJ", 0, 1))
+    ts(("WI", 0, 40), ("DV", 0, 40), ("PF", 0, 1), AL.add)
+    ts(("RL", 0, 48), ("RI", 0, 48), qc, AL.subtract)
+    ts(("LC", 0, 1), qc, 0.0, AL.add)
+    ts(("VC", 0, 1), qc, -8.0, AL.mult, float(TOK - 1 - Z), AL.add)
+    for o in range(2):
+        ts(("WI", 40 + 40 * o, 80 + 40 * o), ("WI", 0, 40), qc, AL.subtract, float(1 + G * o), AL.is_equal)
+    ts(("VC", 0, 1), ("PF", 0, 1), 7.0, AL.mult, ("VC", 0, 1), AL.add)
+    ts(("VAL", 0, TOK), ("DV", 0, TOK), -1.0, AL.mult, ("VC", 0, 1), AL.add)
+    qz("XQ", 0, 2 * TOK, "X12")
+    for t in range(1, R):
+        for k in "cs":
+            x = ("XQ" + k, TOK * (t - 1), TOK * t)
+            send([(enear, "h%s%d" % (k, t), x, [(hand[k], x)])])
+    iota(("IDT", 0, Z), [[TOK, NR], [1, 128]], 0, 0)
     blank(0)
-    qz("E25Q", 0, 512, "E25")
     qz("WQ", 0, 128, "WT")
-    fill(("IDT", Z, Z + 1), -1.0)
+    if me == 0:
+        pick("CA", G * rank, "CM0", CA_, CA_ + G, "LC", 0, 1)
+    qz("E25Q", 0, 512, "E25")
+    fill(("NEW",) + rest, 0.0)
+    for x, c in ((("NEG", 0, 128), -1e29), (("RB", 0, 136 * NB, 136), -1e29), (("WL", 0, 4 * NB), 0), (("TO", 0, 80), 0), (("NGB", 0, TOK), -1e29),
+                 (("SB", 0, 32), 0), (("SB", 32 * TOK, 32 * TOK + 32), 0), (("CP", 0, 4 * NB), 0), (("IDT", Z, Z + 1), -1),
+                 (("WN", 128, 256), 0), (("YS", 16, 144), 0)):
+        put(x, c)
+    for o in range(2):
+        put(("TO", 40 * o + 1 + G * o, 40 * o + 1 + G * o + G), BIG)
+        put(("OG", 104 * o, 104 * o + 1), (CAPP + 1) * BIG)
+    for t in range(R):
+        if t % 2 == me or t + 1 == R:
+            put(("NN%d" % t, 0, 4), 0)
+    for b in range(4):
+        act(("BQ", b, b + 1), qc, AF.Identity, bias=float(32 * b + G * me))
     old(0)
 
-    def none(n):
-        ts(("FF", 0, 2), n, Z - 0.5, AL.is_ge, 128.0, AL.mult)
-
     def flags(n, now):
+        ts(("FF", 0, 2), n, -0.5, AL.is_gt, 128.0, AL.mult)
+        if now:
+            ts(("IL", 0, 4, 2), n, float(Z), AL.add)
         ts(("OS", 0, 4), ("BQ", 0, 4), ("FF", 0, 1), AL.add)
         if now:
             ts(("YL", 0, 1), qc, ("FF", 1, 2), AL.add)
         take("v", ("HC", 0, 64), ("WN", 0, 256), ("OS", 0, 4))
-        if now:
-            cp(("IL", 0, 4, 2), n)
 
     def numbers(t):
         for i in range(2):
             take("s", ("ID", 32 * t + i, 32 * t + 32, 2), ("IDT", 0, Z + 1), ("IL", 2 * i, 2 * i + 1))
-        dma("y", T.ids[:, 32 * t:32 * t + 32], T.ID[0:1, 32 * t:32 * t + 32], [("ID", 32 * t, 32 * t + 32)], [])
 
-    def results(t, q):
+    def results(t):
         act(("YS", 0, G), ("PS", 3584 + G, 3584 + 2 * G), AF.Copy)
         act(("YO", 32 * t, 32 * t + 32, 2), ("PS", 3584, 3584 + G), AF.Copy)
         take("s", ("YO", 32 * t + 1, 32 * t + 32, 2), ("YS", 0, 144), ("YL", 0, 1))
-        dma(q, T.y[:, 32 * t:32 * t + 32], T.YO[:, 32 * t:32 * t + 32], [("YO", 32 * t, 32 * t + 32)], [])
+
+    def store_ids(t):
+        dma("y", T.ids[:, 32 * t:32 * t + 32], T.ID[0:1, 32 * t:32 * t + 32], [("ID", 32 * t, 32 * t + 32)], [])
+
+    def store_y(t):
+        dma("y", T.y[:, 32 * t:32 * t + 32], T.YO[:, 32 * t:32 * t + 32], [("YO", 32 * t, 32 * t + 32)], [])
 
     def stores(t):
-        wait("y", (done["s"], cnt["s"]))
-        numbers(t)
-        results(t, "y")
+        store_ids(t)
+        store_y(t)
 
     def move(t):
-        pk = "PK%d" % t
+        pk, final = "PK%d" % t, t + 1 == R
         for b in range(2):
             mm(b, "E25Q", 128 * b, pk, 0)
+        if final:
+            mm(7, "WQ", 0, pk, 0)
         for b in range(2, 4):
             mm(b, "E25Q", 128 * b, pk, 16, True, False)
             mm(b, "E25Q", 128 * b, pk, 0, False, True)
-        mm(7, "WQ", 0, pk, 0)
+        if not final:
+            mm(7, "WQ", 0, pk, 0)
         for f, b in (("h", 0), ("h", 1), ("n", 0), ("n", 1), ("n", 2), ("n", 3)):
             c, h = 16 * b, ("PS", 512 * b, 512 * b + 16)
             if f == "h":
                 act(("SS", c, c + 16), ("PS", 512 * b + 16, 512 * b + 32), AF.Copy)
                 tt(("HB", c, c + 16), h, ("SS", c, c + 16), AL.add)
-                if b == 1 and t + 1 == R:
+                if b == 1 and final:
+                    results(t)
+                    store_y(t)
                     numbers(t)
+                    store_ids(t)
             else:
                 tt(("NEW", e0 + b, e0 + 64, 4), h if b >= 2 else ("HB", c, c + 16), ("HC", c, c + 16), AL.add)
         qz("CM%d" % (t + 1), q0, 128, "NEW")
@@ -444,53 +453,48 @@ def rank_program(g, core, T, topo):
         scan(("RB", r + 1, r + 1 + n), ("PS", 512 * b, 512 * b + n), ("NEG", 0, n), -1e29, AL.max, AL.max)
         act(("J", 40 * b, 40 * b + 33), ("RB", r + a, r + a + 33), AF.Sign, bias=("RB", r + n, r + n + 1), scale=-1.0, acc=("WL", 4 * b, 4 * b + 1))
 
-    def admit(t, both, ix):
-        tk, hv = "TK%d" % t, ("HV", 0, TOK)
-        best = {0: (AL.min, AL.max), 1: (AL.max, AL.min)}
-        w, v = ("TH", 0, 40), ("VAL", 0, TOK)
-        op("v", lambda e: e.tensor_tensor(view(hv), view(w).indirect(view(ix)), view(v), AL.mult), [w, ix, v], [hv])
-        for o in both:
-            w2, f, a = ("TO", 40 * o, 40 * o + 40), ("OG", 104 * o + 1, 104 * o + 1 + TOK), ("TT", o, o + 1)
-            op("s", lambda e, w2=w2, f=f, a=a: e.activation(view(f), view(w2).indirect(view(ix)), AF.Identity, accum_out=view(a)), [w2, ix], [f, a])
-        steps = []
-        for o in both:
-            cap = ("CAP", TOK * o, TOK * o + TOK)
-            steps.append([
-                lambda o=o, cap=cap: scan(cap, ("NGB", 0, TOK), ("OG", 104 * o, 104 * o + TOK), ("TT", o, o + 1), AL.max, AL.subtract),
-                lambda o=o, cap=cap: scan(("SB", 32 + 8 * o, 32 * 97, 32), hv, cap, 0.0, best[o][0], best[o][1]),
-                lambda o=o: scan(("SB", 48 + 8 * o, 32 * 97, 32), hv, ("SB", 8 * o, 32 * TOK, 32), 0.0, best[o][0], best[o][1])])
-        for i, j in ((0, 0), (0, 1), (1, 0), (0, 2), (1, 1), (1, 2)):
-            if i < len(both):
-                steps[i][j]()
-        turn(("Y1", 0, 32), ("SB", 32 * TOK, 32 * TOK + 32))
-        y1, y2, dl, sg = ("Y1", 0, 32), ("Y2", 0, 64), ("DL", 0, 4), ("SG", 0, 1)
-        op("v", lambda e: e.tensor_scalar(view(y2), view(y1).indirect(view(dl)), view(sg), float(Z), AL.mult, AL.add), [y1, dl, sg], [y2])
-        turn(("RR", 0, 64), y2)
-        shift = {"v": cp, "s": lambda o, i: act(o, i, AF.Copy)}
+    shift = {"v": cp, "s": lambda o, i: act(o, i, AF.Copy)}
+
+    def admit(t, ix, owners):
+        tk, a, n = "TK%d" % t, 32 * TOK, len(owners)
+        at = [n - 1 - i for i in range(n)]
+        for o, j in zip(owners, at):
+            w, v, hv = ("WI", 40 + 40 * o, 80 + 40 * o), ("VAL", 0, TOK), ("HV", TOK * j, TOK * j + TOK)
+            op("v", lambda e, w=w, v=v, hv=hv: e.tensor_tensor(view(hv), view(w).indirect(view(ix)), view(v), AL.mult), [w, ix, v], [hv])
+            w, f, u = ("TO", 40 * o, 40 * o + 40), ("OG", 104 * j + 1, 104 * j + 1 + TOK), ("TT", j, j + 1)
+            op("s", lambda e, w=w, f=f, u=u: e.activation(view(f), view(w).indirect(view(ix)), AF.Identity, accum_out=view(u)), [w, ix], [f, u])
+        for j in at:
+            scan(("CAP", TOK * j, TOK * j + TOK), ("NGB", 0, TOK), ("OG", 104 * j, 104 * j + TOK), ("TT", j, j + 1), AL.max, AL.subtract)
+        for j in at:
+            scan(("SB", 32 + 8 * j, a + 32, 32), ("HV", TOK * j, TOK * j + TOK), ("CAP", TOK * j, TOK * j + TOK), 0.0, AL.min, AL.max)
+        for j in at:
+            scan(("SB", 48 + 8 * j, a + 32, 32), ("HV", TOK * j, TOK * j + TOK), ("SB", 8 * j, a, 32), 0.0, AL.min, AL.max)
         for u in range(2):
-            shift["vs"[u]](("RR", 64, 128, 8, 64 * u, 64 * u + 64), ("RR", 0, 64, 8, 64 - 64 * u, 128 - 64 * u))
+            turn(("Y2", 32 * u, 32 * u + 32), ("SB", a, a + 32))
+        turn(("SB", a + 32, a + 64), ("Y2", G, G + 32))
+        st = G // n
+        for u in range(2):
+            shift["vs"[u]](("SB", a + 64, a + 128, st, 64 * u, 64 * u + 64), ("SB", a, a + 64, st, 64 - 64 * u, 128 - 64 * u))
         for u in range(4):
-            shift["vs"[u // 2]](("RR", 128, 256, 8, 32 * u, 32 * u + 32), ("RR", 0, 128, 8, 32 * (u ^ 1), 32 * (u ^ 1) + 32))
-        nn, of, at = "NN%d" % t, "OF%d" % t, {me: 0, 1 - me: 2}
-        for o in both:
-            scan((nn, 4 + at[o], 68, 4), ("RR", 8 * o, 256, 16), ("ZC", 0, G), float(Z), AL.min, AL.min)
-        for o in both:
-            scan((nn, 5 + at[o], 68, 4), ("RR", 8 * o, 256, 16), (nn, at[o], 64, 4), float(Z), AL.min, AL.max)
-        if len(both) > 1:
+            shift["vs"[u // 2]](("SB", a + 128, a + 256, st, 32 * u, 32 * u + 32), ("SB", a, a + 128, st, 32 * (u ^ 1), 32 * (u ^ 1) + 32))
+        nn, of = "NN%d" % t, "OF%d" % t
+        for j in at:
+            act(("JS", G * j, G * j + G), ("SB", a + 8 * j, a + 256, G), AF.Relu, scale=-BIG, acc=("SU", j, j + 1))
+            scan((nn, 4 + 2 * j, 68, 4), ("SB", a + 8 * j, a + 256, G), ("ZT", 0, G), 0.0, AL.min, AL.min)
+        for j in at:
+            scan((nn, 5 + 2 * j, 68, 4), ("SB", a + 8 * j, a + 256, G), (nn, 2 * j, 64, 4), 0.0, AL.min, AL.max)
+        if n > 1:
             send([(eall, "aL%d" % t, (nn, 66, 68), [(T.cores[mate], ("LN%d" % t, 0, 2))])])
-        w3 = 2 * len(both)
-        cp((of, 0, w3, 2), (nn, 64, 64 + w3, 2))
-        ts(("KK", 0, len(both)), (nn, 65, 64 + w3, 2), Z - 0.5, AL.is_ge, -BIG, AL.mult)
-        none((nn, 64, 66))
-        for o in both:
-            c = at[o]
-            ts((of, c + 1, c + 2), ("KK", c // 2, c // 2 + 1), (nn, 65 + c, 66 + c), AL.add, (nn, 64 + c, 65 + c), AL.max)
-        pick("PK%d" % t, 0, tk, 0, Z + 128, of, 0, w3)
-        if len(both) > 1:
+        for j in at:
+            ts(("KK", j, j + 1), (nn, 64 + 2 * j, 65 + 2 * j), BIG + 1, AL.mult, ("SU", j, j + 1), AL.add)
+        ts((of, 0, 2 * n, 2), (nn, 64, 64 + 2 * n, 2), float(Z), AL.add)
+        for j in at:
+            ts((of, 2 * j + 1, 2 * j + 2), ("KK", j, j + 1), (nn, 65 + 2 * j, 66 + 2 * j), AL.min, float(Z), AL.add)
+        pick("PK%d" % t, 0, tk, 0, Z + 128, of, 0, 2 * n)
+        if n > 1:
             for k in "cs":
                 send([(eall, "aK%d" % t, ("PK%d%s" % (t, k), 32, 64), [(T.cores[mate], ("PK%d%s" % (t, k), 0, 32))])])
 
-    late = []
     for t in range(R):
         tk, final = "TK%d" % t, t + 1 == R
         ix, n = ("IX", 0, NB), ("NN%d" % t, 64, 66)
@@ -506,78 +510,78 @@ def rank_program(g, core, T, topo):
                     winner(b, 128, G * pair[0])
                 cp(ix, ("WL", 0, 4 * NB, 4))
             else:
-                m = ("MX%d" % t, 0, NB)
+                m, far = ("MX%d" % t, 0, NB), _far(rank, t, T, topo)
                 for b in range(NB):
                     mm(b, "RP", 128 * b, "CM%d" % t, CA_)
                 for b in range(NB):
                     i, o = ("PS", 512 * b, 512 * b + 2 * G), ("MX%d" % t, b, b + 1)
                     op("v", lambda v, i=i, o=o: v.tensor_reduce(view(o), view(i), AX, AL.max), [i], [o])
-                sc = _scorers(t, T, topo)
-
-                def slot(s, d):
-                    i = [r for r in sc if r != d].index(s)
-                    return ("MR%d" % t, 8 * i, 8 * i + NB)
-
-                send([(efar, "aM%d" % t, m, [(T.cores[r], slot(rank, r)) for r in _far(rank, t, T, topo)])])
+                for i, r in enumerate(far):
+                    send([(efar, "aM%d%d" % (t, i), m, [(T.cores[r], ("MR%d" % t, 8 * i, 8 * i + NB))])])
                 for b in range(NB):
                     winner(b, 2 * G, 0)
                 old(t)
-                for f in late:
-                    f()
-                late = []
-                for i, r in enumerate([r for r in sc if r != rank]):
-                    tt(("CP", 1 + i, 4 * NB, 4), m, slot(r, rank), AL.is_gt if r < rank else AL.is_ge)
+                numbers(t - 1)
+                results(t - 1)
+                for i, r in enumerate(far[::-1]):
+                    tt(("CP", 1 + i, 4 * NB, 4), m, ("MR%d" % t, 8 * i, 8 * i + NB), AL.is_gt if r < rank else AL.is_ge)
                 scan(("PR", 0, 4 * NB), ("CP", 0, 4 * NB), ("WL", 0, 4 * NB), 0.0, AL.mult, AL.add)
                 cp(ix, ("PR", 3, 4 * NB, 4))
             if final:
                 send([(eall, "aL%d" % t, ix, [(T.cores[mate], ("IY", 0, NB))])])
-            admit(t, (me,) if final else (1 - me, me), ix)
+                wait("y", (done["v"], cnt["v"] + 3))
+                stores(t - 1)
+                admit(t, ix, [me])
+            else:
+                if t > 0:
+                    wait("y", (done["v"], cnt["v"]))
+                    stores(t - 1)
+                admit(t, ix, [1 - me, me])
             flags(n, final)
             move(t)
-            if final:
-                results(t, "s")
-            else:
+            if not final:
                 for k in "cs":
                     x = ("CM%d%s" % (t + 1, k), co, co + G)
                     send([(eall, "aN%d" % (t + 1), x, [(T.cores[mate], x)])])
                 ts(("YL", 0, 1), qc, ("FF", 1, 2), AL.add)
-                cp(("IL", 0, 4, 2), n)
-        elif final:
-            blank(t)
-            old(t)
-            stores(t - 1)
-            admit(t, (me,), ("IY", 0, NB))
-            flags(n, True)
-            move(t)
-            results(t, "s")
+                ts(("IL", 0, 4, 2), n, float(Z), AL.add)
         else:
             if t > 0:
                 blank(t)
                 old(t)
+                numbers(t - 1)
+                results(t - 1)
                 stores(t - 1)
-            blank(t + 1)
-            qz("TK%d" % (t + 1), 128 * rank, 128, "X12", 4 * TOK * t)
-            if t + 2 == R:
-                for k in "cs":
-                    send([(eall[share * i:share * i + share], "aT%s%d" % (k, t + 1), tokens(t + 1, k, r), [(T.cores[mate], tokens(t + 1, k, r))])
-                          for i, r in enumerate([r for r in range(NR) if r != mate])])
+            if final:
+                admit(t, ("IY", 0, NB), [me])
+                flags(n, True)
             else:
-                qz("TK%d" % (R - 1), 128 * rank, 128, "X12", 4 * TOK * (R - 2))
-            pick("RP", 0, "TK%d" % (t + 1), 0, Z + 128, "RL", 0, 8 * NB)
-            none(("LN%d" % t, 0, 2))
-            flags(("LN%d" % t, 0, 2), True)
+                nx = "TK%d" % (t + 1)
+                blank(t + 1)
+                qz(nx, 128 * rank, 128, "X12", 4 * TOK * t)
+                if t + 2 == R:
+                    for k in "cs":
+                        es, w = share[k]
+                        send([(es[w * i:w * i + w], "aT%s%d" % (k, t + 1), tokens(t + 1, k, r), [(T.cores[mate], tokens(t + 1, k, r))])
+                              for i, r in enumerate([r for r in range(NR) if r != mate])])
+                else:
+                    qz("TK%d" % (R - 1), 128 * rank, 128, "X12", 4 * TOK * (R - 2))
+                for a in (0, 4 * NB):
+                    pickc("RP", 16 * a, nx, 0, Z + 128, "RL", a, a + 4 * NB)
+                for q, a in (("s", 0), ("v", 4 * NB)):
+                    picks(q, "RP", 16 * a, nx, 0, Z + 128, "RL", a, a + 4 * NB)
+                flags(("LN%d" % t, 0, 2), True)
             move(t)
-            late = [lambda t=t: numbers(t), lambda t=t: results(t, "y")]
     hn = "CM%d" % R
     i = (hn + "c", co, co + G)
     dma("y", T.oc[:, 0:4 * G], view(i).bitcast(dt.uint8), [i], [])
     for k in range(4):
-        dma("ys"[k % 2], T.osc[4 * k:4 * k + 4, 0:G], T[hn + "s"][32 * k:32 * k + 4, co:co + G], [(hn + "s", co, co + G)], [])
+        dma("ssys"[k], T.osc[4 * k:4 * k + 4, 0:G], T[hn + "s"][32 * k:32 * k + 4, co:co + G], [(hn + "s", co, co + G)], [])
 
+    for tok in outer:
+        wait("g", tok)
+    g.wait_ge(T.sem.sent, sent[0])
     for q in cnt:
         wait("g", (done[q], cnt[q]))
     for i in range(nd[0]):
         wait("g", ("d%d" % i, 16))
-    for tok in outer:
-        wait("g", tok)
-    g.wait_ge(T.sem.sent, sent[0])

from concourse.bass import DstId, RemoteDMATransfer
from concourse.mybir import dt, AluOpType, AxisListType, ActivationFunctionType

G, TOK, CAPP, R, NR = 16, 96, 48, 3, 8
NB = TOK // G
Z = 128 * NR
BIG = 2048.0
CA_ = 128
BY = {"c": 3, "s": 2}

F32, BF, I32, U16, COD, PLN = "float32", "bfloat16", "int32", "uint16", "float8_e4m3fn_x4", "uint8"
SCRATCH = {"PS": ("psum", [128, 4096], F32)}
SEMAPHORES = ["vd", "sd", "pd", "gd", "sent", "aC", "gc", "gs", "hc1", "hs1", "hc2", "hs2"]


def _buf(name, n, dtype):
    SCRATCH[name] = ("sbuf", [128, n], dtype)


def _mx(name, n):
    _buf(name + "c", n, COD)
    _buf(name + "s", n, PLN)


for _n, _w in (("CBT", 512), ("X0", 512), ("X12", 896), ("WT", 512), ("ZT", 512), ("E25", 2048), ("NEW", 512), ("J", 40 * NB),
               ("NGB", TOK), ("OG", 208), ("CAP", 2 * TOK)):
    _buf(_n, _w, BF)
for _n, _w in (("NEG", 128), ("AB", 128), ("DV", 128), ("QC", 1), ("PF", 1), ("VC", 1), ("WI", 120), ("TO", 80), ("VAL", TOK),
               ("RB", 136 * NB), ("WL", 4 * NB), ("CP", 4 * NB), ("PR", 4 * NB), ("HV", 2 * TOK), ("JS", 2 * G), ("SU", 2), ("TT", 2),
               ("SB", 32 * 104), ("Y2", 64), ("KK", 2), ("FF", 2), ("SS", 64), ("HB", 64), ("WN", 256), ("HC", 64), ("BQ", 4),
               ("YO", 96), ("YS", 144), ("IDT", Z + 8), ("ID", 96)):
    _buf(_n, _w, F32)
for _n, _w in (("QI", 1), ("QJ", 1), ("RI", 48)):
    _buf(_n, _w, I32)
for _n, _w in (("RL", 48), ("LC", 2), ("IX", 6), ("IY", 6), ("OS", 4), ("YL", 2), ("IL", 4)):
    _buf(_n, _w, U16)
for _n, _w in (("XQ", 192), ("WQ", 128), ("E25Q", 512), ("CA", 128), ("RP", 128 * NB)):
    _mx(_n, _w)
for _t in range(R):
    _mx("TK%d" % _t, Z + 128)
    _mx("PK%d" % _t, 192)
    _buf("NN%d" % _t, 68, F32)
    _buf("LN%d" % _t, 2, F32)
    _buf("MX%d" % _t, 8, F32)
    _buf("MR%d" % _t, 24, F32)
    _buf("OF%d" % _t, 4, U16)
    SEMAPHORES += ["aTc%d" % _t, "aTs%d" % _t, "aL%d" % _t, "aK%d" % _t, "aN%d" % _t] + ["aM%d%d" % (_t, _i) for _i in range(3)]
for _t in range(R + 1):
    _mx("CM%d" % _t, 288)
SEMAPHORES += ["d%d" % _i for _i in range(24)]


def _bits(es):
    return sum(1 << e for e in es)


def _helper_of(core, T, topo, i):
    return [c for c in topo.cores_of(core) if T.rank_of(c) is None and topo.die(c) == topo.die(core)][i]


def _dst(c, topo):
    a = topo.addr(c)
    return DstId(rid=a[0], pnc=a[1])


def _pair(rank, T, topo):
    return [r for r in range(len(T.cores)) if topo.chip(T.cores[r]) == topo.chip(T.cores[rank])]


def _scorers(t, T, topo):
    return [r for r in range(len(T.cores)) if _pair(r, T, topo)[t % 2] == r]


def _far(rank, t, T, topo):
    n = len(T.cores)
    return [r for r in [(rank + i) % n for i in range(1, n)] if r in _scorers(t, T, topo) and r not in _pair(rank, T, topo)]


def _near_engines(a, b, far, topo):
    return [e for e in topo.engines(a, b) if e not in topo.engines(a, far)]


def _hand_on(g, core, rank, T, topo, k):
    me = T.cores[rank]
    other = T.cores[_far(rank, 0, T, topo)[0]]
    es, en = topo.engines(core, other), _near_engines(core, me, other, topo)
    came = len(_near_engines(me, core, other, topo))
    byt = (lambda v: v.bitcast(dt.uint8)) if k == "c" else (lambda v: v)
    pair = _pair(rank, T, topo)
    n = [0]

    def on(sets, sem, src, dst):
        g.remote_dma_fused([RemoteDMATransfer(dst_ids=[_dst(T.cores[r], topo) for r in rs], dma_engine_mask=_bits(e), remote_sem=T.sem[sem],
                                              srcs=[byt(src)], dsts=[byt(dst)] * len(rs)) for e, rs in sets], local_sem=T.sem.sent)
        n[0] += sum(len(e) for e, _ in sets)

    def sets(t):
        return [(es, _far(rank, t, T, topo))] + ([(en, [pair[t % 2]])] if pair[t % 2] != rank else [])

    o = CA_ + G * pair.index(rank)
    g.wait_ge(T.sem["g" + k], came)
    for e, rs in sets(0):
        on([(e, rs[:BY[k]])], "aC", T["CM0" + k][:, o:o + G], T["CA" + k][:, G * rank:G * rank + G])
    for t in range(1, R):
        g.wait_ge(T.sem["h%s%d" % (k, t)], came)
        if t > 1:
            g.wait_ge(T.sem.sent, n[0])
        on(sets(t), "aT%s%d" % (k, t), T["XQ" + k][:, TOK * (t - 1):TOK * t], T["TK%d%s" % (t, k)][:, 128 * rank:128 * rank + TOK])
    g.wait_ge(T.sem.sent, n[0])


def rank_program(g, core, T, topo):
    rank = T.rank_of(core)
    if rank is None:
        for r in range(len(T.cores)):
            for i, k in enumerate("cs"):
                if _helper_of(T.cores[r], T, topo, i) == core:
                    _hand_on(g, core, r, T, topo, k)
        return
    AL, AF, AX = AluOpType, ActivationFunctionType, AxisListType.X
    pair = _pair(rank, T, topo)
    me = pair.index(rank)
    mate = pair[1 - me]
    co = CA_ + G * me
    q0 = co + G - 128 if me == 0 else co
    e0 = 4 * (co - q0)
    eng = {"v": g.vector, "s": g.scalar, "p": g.tensor, "g": g, "y": g.sync}
    done = {"v": "vd", "s": "sd", "p": "pd", "g": "gd"}
    cnt, seen, log, nd = {}, {}, {}, [0]

    def cols(x):
        nm, a, b = x[0], x[1], x[2]
        st = x[3] if len(x) > 3 else 1
        if nm == "PS":
            return nm, frozenset(range(a // 512, (b - 1) // 512 + 1))
        qs = range(x[4] // 32, x[5] // 32) if len(x) > 4 else range(4)
        return nm, frozenset(4 * c + u for c in range(a, b, st) for u in qs)

    def view(x):
        st = x[3] if len(x) > 3 else 1
        p0, p1 = (x[4], x[5]) if len(x) > 4 else (0, 128)
        if len(x) > 4:
            return T[x[0]][p0:p1, x[1]:x[2]:st]
        return T[x[0]][:, x[1]:x[2]] if st == 1 else T[x[0]][:, x[1]:x[2]:st]

    def wait(q, tok):
        if seen.get((q, tok[0]), 0) < tok[1]:
            eng[q].wait_ge(T.sem[tok[0]], tok[1])
            seen[(q, tok[0])] = tok[1]

    def before(q, rd, wr):
        best = {}
        for kind, xs in (("r", rd), ("w", wr)):
            for x in xs:
                nm, cs = cols(x)
                for k, c2, tok, q2 in log.get(nm, []):
                    clash = kind == "w" or k == "w" or (nm == "PS" and q2 != q)
                    if clash and cs & c2 and not (q == "p" and q2 == "p"):
                        best[tok[0]] = max(best.get(tok[0], 0), tok[1])
        for s in sorted(best):
            wait(q, (s, best[s]))

    def after(q, tok, rd, wr):
        for x in wr:
            nm, cs = cols(x)
            log[nm] = [e for e in log.get(nm, []) if not e[1] <= cs] + [("w", cs, tok, q)]
        for x in rd:
            nm, cs = cols(x)
            log.setdefault(nm, []).append(("r", cs, tok, q))

    def op(q, f, rd, wr):
        before(q, rd, wr)
        cnt[q] = cnt.get(q, 0) + 1
        tok = (done[q], cnt[q])
        f(eng[q]).then_inc(T.sem[tok[0]], 1)
        after(q, tok, rd, wr)
        return tok

    def isap(x):
        return isinstance(x, tuple)

    def ts(out, in0, s1, op0, s2=None, op1=None):
        sc = [view(s) if isap(s) else s for s in (s1, s2)]
        rd = [in0] + [s for s in (s1, s2) if isap(s)]
        if op1 is None:
            return op("v", lambda v: v.tensor_scalar(view(out), view(in0), sc[0], None, op0), rd, [out])
        return op("v", lambda v: v.tensor_scalar(view(out), view(in0), sc[0], sc[1], op0, op1), rd, [out])

    def tt(out, a, b, o):
        return op("v", lambda v: v.tensor_tensor(view(out), view(a), view(b), o), [a, b], [out])

    def cp(out, a):
        return op("v", lambda v: v.tensor_copy(view(out), view(a)), [a], [out])

    def act(out, a, f, bias=0.0, scale=1.0, acc=None):
        rd = [a] + [x for x in (bias, scale) if isap(x)]
        b, c = [view(x) if isap(x) else x for x in (bias, scale)]
        if acc is not None:
            return op("s", lambda s: s.activation(view(out), view(a), f, bias=b, scale=c, accum_out=view(acc)), rd, [out, acc])
        if f == AF.Copy:
            return op("s", lambda s: s.activation(view(out), view(a), f, scale=c), rd, [out])
        return op("s", lambda s: s.activation(view(out), view(a), f, bias=b, scale=c), rd, [out])

    def take(q, out, win, of):
        if q == "v":
            return op("v", lambda v: v.tensor_copy(view(out), view(win).indirect(view(of))), [win, of], [out])
        return op("s", lambda s: s.activation(view(out), view(win).indirect(view(of)), AF.Copy), [win, of], [out])

    def fill(x, c):
        return op("v", lambda v: v.memset(view(x), c), [], [x])

    def scan(out, d0, d1, ini, o0, o1):
        i = view(ini) if isap(ini) else ini
        return op("v", lambda v: v.tensor_tensor_scan(view(out), view(d0), view(d1), i, o0, o1), [d0, d1] + ([ini] if isap(ini) else []), [out])

    def turn(out, a):
        return op("v", lambda v: v.transpose(view(out), view(a)), [a], [out])

    def qz(nm, a, n, tile, ta=0):
        oc, os_, i = (nm + "c", a, a + n), (nm + "s", a, a + n), (tile, ta, ta + 4 * n)
        return op("v", lambda v: v.quantize_mx(view(oc), view(os_), view(i)), [i], [oc, os_])

    def mm(bank, st, sa, mv, ma, start=True, stop=True):
        o = ("PS", 512 * bank, 512 * bank + 128)
        a, b = (st + "c", sa, sa + 128), (st + "s", sa, sa + 128)
        c, d = (mv + "c", ma, ma + 128), (mv + "s", ma, ma + 128)
        return op("p", lambda p: p.matmul_mx(view(o), view(a), view(b), view(c), view(d), start, stop), [a, b, c, d], [o])

    def pickc(dst, da, src, wa, wb, of, oa, ob):
        o, w, f = (of, oa, ob), (src + "c", wa, wb), (dst + "c", da, da + 16 * (ob - oa))
        op("v", lambda v: v.tensor_copy(view(f).bitcast(dt.uint32), view(w).bitcast(dt.uint32).indirect(view(o))), [w, o], [f])

    def picks(q, dst, da, src, wa, wb, of, oa, ob):
        take(q, (dst + "s", da, da + 16 * (ob - oa)), (src + "s", wa, wb), (of, oa, ob))

    def pick(dst, da, src, wa, wb, of, oa, ob):
        pickc(dst, da, src, wa, wb, of, oa, ob)
        picks("s", dst, da, src, wa, wb, of, oa, ob)

    def dma(q, out, in_, rd, wr):
        before(q, rd, wr)
        tok = ("d%d" % nd[0], 16)
        nd[0] += 1
        eng[q].dma_start(out, in_).then_inc(T.sem[tok[0]], 16)
        after(q, tok, rd, wr)

    def iota(x, pat, base, ch):
        if SCRATCH[x[0]][2] == I32:
            op("g", lambda e: e.iota(view(x), pat, base, ch), [], [x])
        else:
            op("g", lambda e: e.iota(view(x), pat, base, ch, allow_small_or_imprecise_dtypes=True), [], [x])

    outer = []

    def ext(sem, val, xs):
        outer.append((sem, val))
        for x in xs:
            nm, cs = cols(x)
            log.setdefault(nm, []).append(("w", cs, (sem, val), "x"))

    peers = [r for r in range(NR) if r != rank]
    far0 = _far(rank, 0, T, topo)
    other = T.cores[far0[0]]
    efar, eall = topo.engines(core, other), topo.engines(core, T.cores[mate])
    enear = _near_engines(core, T.cores[mate], other, topo)
    hand = {"c": _helper_of(core, T, topo, 0), "s": _helper_of(core, T, topo, 1)}
    share = {"c": (eall, len(eall) // NR), "s": (enear, len(enear) // NR)}
    sent = [0]

    def send(transfers):
        tr, rd = [], []
        for es, sem, src, dsts in transfers:
            code = SCRATCH[src[0]][2] == COD
            b = (lambda v: v.bitcast(dt.uint8)) if code else (lambda v: v)
            tr.append(RemoteDMATransfer(dst_ids=[_dst(c, topo) for c, _ in dsts], dma_engine_mask=_bits(es), remote_sem=T.sem[sem],
                                        srcs=[b(view(src))], dsts=[b(view(x)) for _, x in dsts]))
            rd.append(src)
            sent[0] += len(es)
        before("g", rd, [])
        g.remote_dma_fused(tr, local_sem=T.sem.sent)

    def tokens(t, k, r):
        return ("TK%d%s" % (t, k), 128 * r, 128 * r + TOK)

    dma("s", T.X0[:, 0:4 * TOK], T.x[:, 0:4 * TOK], [], [("X0", 0, 4 * TOK)])
    dma("y", T.CBT[:, e0:e0 + 4 * G], T.cb[:], [], [("CBT", e0, e0 + 4 * G)])
    dma("y", T.X12[:, 0:8 * TOK], T.x[:, 4 * TOK:12 * TOK], [], [("X12", 0, 8 * TOK)])
    dma("s", T.WT[:], T.w[:], [], [("WT", 0, 512)])
    iota(("DV", 0, 128), [[1, 128]], 0, -1)
    iota(("QI", 0, 1), [[0, 1]], 0, 1)
    iota(("RI", 0, 48), [[-G, NB], [128, NR]], TOK - 1, 0)
    rest = (0, e0) if me == 0 else (4 * G, 512)
    dv, qc = ("DV", 0, 128), ("QC", 0, 1)
    fill(("X0", 4 * TOK, 512), 0.0)
    fill(("CBT",) + rest, 0.0)
    fill(("ZT", 0, 512), 0.0)
    fill(("X12", 8 * TOK, 896), 0.0)
    qz("TK0", 128 * rank, 128, "X0")
    qz("CM0", q0, 128, "CBT")

    def first(k):
        x = tokens(0, k, rank)
        send([(efar, "aT%s0" % k, x, [(T.cores[r], x) for r in far0])])

    first("c")
    for k in "cs":
        x = ("CM0" + k, co, co + G)
        send([(enear, "g" + k, x, [(hand[k], x)])])
    first("s")
    for k in "cs":
        for r in far0[BY[k]:]:
            send([(efar, "aC", ("CM0" + k, co, co + G), [(T.cores[r], ("CA" + k, G * rank, G * rank + G))])])
    if me == 1:
        for k in "cs":
            x = tokens(0, k, rank)
            send([(enear, "aT%s0" % k, x, [(T.cores[mate], x)])])
    came = len(efar) * (NR - 2) + len(enear)
    for t in range(R):
        if t % 2 == me:
            for k in "cs":
                ext("aT%s%d" % (k, t), came, [tokens(t, k, r) for r in peers])
            if t == 0:
                ext("aC", 2 * came, [("CA" + k, G * r, G * r + G) for k in "cs" for r in peers])
            else:
                for i in range(3):
                    ext("aM%d%d" % (t, i), len(efar), [("MR%d" % t, 8 * i, 8 * i + NB)])
                o = CA_ + G * (1 - me)
                ext("aN%d" % t, 2 * len(eall), [("CM%d%s" % (t, k), o, o + G) for k in "cs"])
        elif t + 1 < R:
            ext("aL%d" % t, len(eall), [("LN%d" % t, 0, 2)])
            ext("aK%d" % t, 2 * len(eall), [("PK%d%s" % (t, k), 0, 32) for k in "cs"])
        else:
            ext("aL%d" % t, len(eall), [("IY", 0, NB)])
            for k in "cs":
                ext("aT%s%d" % (k, t), share[k][1] * len(peers), [tokens(t, k, r) for r in peers])

    def blank(t):
        lands = t > 0 and t % 2 == me
        qz("CM%d" % t, (CA_ + 2 * G if lands else CA_ + G) if me == 0 else (0 if lands else G), 128, "ZT")
        qz("PK%d" % t, 64 if t % 2 == me and t + 1 < R else 32, 128, "ZT")
        if t % 2 == me or t + 1 == R:
            qz("TK%d" % t, Z, 128, "ZT")

    def old(t):
        for b in range(4):
            mm(6, "E25Q", 128 * b, "CM%d" % t, CA_ - 32 * b, b == 0, b == 3)
        act(("WN", 0, 128), ("PS", 3072, 3200), AF.Copy, scale=2.0)
        for b in range(4):
            c = 128 + 32 * b + G * me
            act(("WN", c, c + G), ("CBT" if t == 0 else "NEW", e0 + b, e0 + 64, 4), AF.Copy)

    def put(x, c):
        n = len(range(x[1], x[2], x[3] if len(x) > 3 else 1))
        act(x, ("ZT", 0, n), AF.Identity, bias=float(c))

    act(("AB", 0, 128), dv, AF.Abs)
    for b in range(4):
        act(("E25", 512 * b, 512 * b + 512), ("ZT", 0, 512), AF.Copy)
    for b in range(4):
        act(("E25", 512 * b + b, 512 * b + 512, 4), ("AB", 0, 128), AF.Relu, bias=0.25, scale=-1.0)
    ts(("QJ", 0, 1), ("QI", 0, 1), 15, AL.bitwise_and)
    cp(("PF", 0, 1), ("QI", 0, 1))
    cp(qc, ("QJ", 0, 1))
    ts(("WI", 0, 40), ("DV", 0, 40), ("PF", 0, 1), AL.add)
    ts(("RL", 0, 48), ("RI", 0, 48), qc, AL.subtract)
    ts(("LC", 0, 1), qc, 0.0, AL.add)
    ts(("VC", 0, 1), qc, -8.0, AL.mult, float(TOK - 1 - Z), AL.add)
    for o in range(2):
        ts(("WI", 40 + 40 * o, 80 + 40 * o), ("WI", 0, 40), qc, AL.subtract, float(1 + G * o), AL.is_equal)
    ts(("VC", 0, 1), ("PF", 0, 1), 7.0, AL.mult, ("VC", 0, 1), AL.add)
    ts(("VAL", 0, TOK), ("DV", 0, TOK), -1.0, AL.mult, ("VC", 0, 1), AL.add)
    qz("XQ", 0, 2 * TOK, "X12")
    for t in range(1, R):
        for k in "cs":
            x = ("XQ" + k, TOK * (t - 1), TOK * t)
            send([(enear, "h%s%d" % (k, t), x, [(hand[k], x)])])
    iota(("IDT", 0, Z), [[TOK, NR], [1, 128]], 0, 0)
    blank(0)
    qz("WQ", 0, 128, "WT")
    if me == 0:
        pick("CA", G * rank, "CM0", CA_, CA_ + G, "LC", 0, 1)
    qz("E25Q", 0, 512, "E25")
    fill(("NEW",) + rest, 0.0)
    for x, c in ((("NEG", 0, 128), -1e29), (("RB", 0, 136 * NB, 136), -1e29), (("WL", 0, 4 * NB), 0), (("TO", 0, 80), 0), (("NGB", 0, TOK), -1e29),
                 (("SB", 0, 32), 0), (("SB", 32 * TOK, 32 * TOK + 32), 0), (("CP", 0, 4 * NB), 0), (("IDT", Z, Z + 1), -1),
                 (("WN", 128, 256), 0), (("YS", 16, 144), 0)):
        put(x, c)
    for o in range(2):
        put(("TO", 40 * o + 1 + G * o, 40 * o + 1 + G * o + G), BIG)
        put(("OG", 104 * o, 104 * o + 1), (CAPP + 1) * BIG)
    for t in range(R):
        if t % 2 == me or t + 1 == R:
            put(("NN%d" % t, 0, 4), 0)
    for b in range(4):
        act(("BQ", b, b + 1), qc, AF.Identity, bias=float(32 * b + G * me))
    old(0)

    def flags(n, now):
        ts(("FF", 0, 2), n, -0.5, AL.is_gt, 128.0, AL.mult)
        if now:
            ts(("IL", 0, 4, 2), n, float(Z), AL.add)
        ts(("OS", 0, 4), ("BQ", 0, 4), ("FF", 0, 1), AL.add)
        if now:
            ts(("YL", 0, 1), qc, ("FF", 1, 2), AL.add)
        take("v", ("HC", 0, 64), ("WN", 0, 256), ("OS", 0, 4))

    def numbers(t):
        for i in range(2):
            take("s", ("ID", 32 * t + i, 32 * t + 32, 2), ("IDT", 0, Z + 1), ("IL", 2 * i, 2 * i + 1))

    def results(t):
        act(("YS", 0, G), ("PS", 3584 + G, 3584 + 2 * G), AF.Copy)
        act(("YO", 32 * t, 32 * t + 32, 2), ("PS", 3584, 3584 + G), AF.Copy)
        take("s", ("YO", 32 * t + 1, 32 * t + 32, 2), ("YS", 0, 144), ("YL", 0, 1))

    def store_ids(t):
        dma("y", T.ids[:, 32 * t:32 * t + 32], T.ID[0:1, 32 * t:32 * t + 32], [("ID", 32 * t, 32 * t + 32)], [])

    def store_y(t):
        dma("y", T.y[:, 32 * t:32 * t + 32], T.YO[:, 32 * t:32 * t + 32], [("YO", 32 * t, 32 * t + 32)], [])

    def stores(t):
        store_ids(t)
        store_y(t)

    def move(t):
        pk, final = "PK%d" % t, t + 1 == R
        for b in range(2):
            mm(b, "E25Q", 128 * b, pk, 0)
        if final:
            mm(7, "WQ", 0, pk, 0)
        for b in range(2, 4):
            mm(b, "E25Q", 128 * b, pk, 16, True, False)
            mm(b, "E25Q", 128 * b, pk, 0, False, True)
        if not final:
            mm(7, "WQ", 0, pk, 0)
        for f, b in (("h", 0), ("h", 1), ("n", 0), ("n", 1), ("n", 2), ("n", 3)):
            c, h = 16 * b, ("PS", 512 * b, 512 * b + 16)
            if f == "h":
                act(("SS", c, c + 16), ("PS", 512 * b + 16, 512 * b + 32), AF.Copy)
                tt(("HB", c, c + 16), h, ("SS", c, c + 16), AL.add)
                if b == 1 and final:
                    results(t)
                    store_y(t)
                    numbers(t)
                    store_ids(t)
            else:
                tt(("NEW", e0 + b, e0 + 64, 4), h if b >= 2 else ("HB", c, c + 16), ("HC", c, c + 16), AL.add)
        qz("CM%d" % (t + 1), q0, 128, "NEW")

    def winner(b, n, a):
        r = 136 * b
        scan(("RB", r + 1, r + 1 + n), ("PS", 512 * b, 512 * b + n), ("NEG", 0, n), -1e29, AL.max, AL.max)
        act(("J", 40 * b, 40 * b + 33), ("RB", r + a, r + a + 33), AF.Sign, bias=("RB", r + n, r + n + 1), scale=-1.0, acc=("WL", 4 * b, 4 * b + 1))

    shift = {"v": cp, "s": lambda o, i: act(o, i, AF.Copy)}

    def admit(t, ix, owners):
        tk, a, n = "TK%d" % t, 32 * TOK, len(owners)
        at = [n - 1 - i for i in range(n)]
        for o, j in zip(owners, at):
            w, v, hv = ("WI", 40 + 40 * o, 80 + 40 * o), ("VAL", 0, TOK), ("HV", TOK * j, TOK * j + TOK)
            op("v", lambda e, w=w, v=v, hv=hv: e.tensor_tensor(view(hv), view(w).indirect(view(ix)), view(v), AL.mult), [w, ix, v], [hv])
            w, f, u = ("TO", 40 * o, 40 * o + 40), ("OG", 104 * j + 1, 104 * j + 1 + TOK), ("TT", j, j + 1)
            op("s", lambda e, w=w, f=f, u=u: e.activation(view(f), view(w).indirect(view(ix)), AF.Identity, accum_out=view(u)), [w, ix], [f, u])
        for j in at:
            scan(("CAP", TOK * j, TOK * j + TOK), ("NGB", 0, TOK), ("OG", 104 * j, 104 * j + TOK), ("TT", j, j + 1), AL.max, AL.subtract)
        for j in at:
            scan(("SB", 32 + 8 * j, a + 32, 32), ("HV", TOK * j, TOK * j + TOK), ("CAP", TOK * j, TOK * j + TOK), 0.0, AL.min, AL.max)
        for j in at:
            scan(("SB", 48 + 8 * j, a + 32, 32), ("HV", TOK * j, TOK * j + TOK), ("SB", 8 * j, a, 32), 0.0, AL.min, AL.max)
        for u in range(2):
            turn(("Y2", 32 * u, 32 * u + 32), ("SB", a, a + 32))
        turn(("SB", a + 32, a + 64), ("Y2", G, G + 32))
        st = G // n
        for u in range(2):
            shift["vs"[u]](("SB", a + 64, a + 128, st, 64 * u, 64 * u + 64), ("SB", a, a + 64, st, 64 - 64 * u, 128 - 64 * u))
        for u in range(4):
            shift["vs"[u // 2]](("SB", a + 128, a + 256, st, 32 * u, 32 * u + 32), ("SB", a, a + 128, st, 32 * (u ^ 1), 32 * (u ^ 1) + 32))
        nn, of = "NN%d" % t, "OF%d" % t
        for j in at:
            act(("JS", G * j, G * j + G), ("SB", a + 8 * j, a + 256, G), AF.Relu, scale=-BIG, acc=("SU", j, j + 1))
            scan((nn, 4 + 2 * j, 68, 4), ("SB", a + 8 * j, a + 256, G), ("ZT", 0, G), 0.0, AL.min, AL.min)
        for j in at:
            scan((nn, 5 + 2 * j, 68, 4), ("SB", a + 8 * j, a + 256, G), (nn, 2 * j, 64, 4), 0.0, AL.min, AL.max)
        if n > 1:
            send([(eall, "aL%d" % t, (nn, 66, 68), [(T.cores[mate], ("LN%d" % t, 0, 2))])])
        for j in at:
            ts(("KK", j, j + 1), (nn, 64 + 2 * j, 65 + 2 * j), BIG + 1, AL.mult, ("SU", j, j + 1), AL.add)
        ts((of, 0, 2 * n, 2), (nn, 64, 64 + 2 * n, 2), float(Z), AL.add)
        for j in at:
            ts((of, 2 * j + 1, 2 * j + 2), ("KK", j, j + 1), (nn, 65 + 2 * j, 66 + 2 * j), AL.min, float(Z), AL.add)
        pick("PK%d" % t, 0, tk, 0, Z + 128, of, 0, 2 * n)
        if n > 1:
            for k in "cs":
                send([(eall, "aK%d" % t, ("PK%d%s" % (t, k), 32, 64), [(T.cores[mate], ("PK%d%s" % (t, k), 0, 32))])])

    for t in range(R):
        tk, final = "TK%d" % t, t + 1 == R
        ix, n = ("IX", 0, NB), ("NN%d" % t, 64, 66)
        if t % 2 == me:
            if t == 0:
                for b in range(NB):
                    pickc("RP", 128 * b, tk, 0, Z + 128, "RL", 8 * b, 8 * b + 8)
                for b in range(NB):
                    picks("ssvsvs"[b], "RP", 128 * b, tk, 0, Z + 128, "RL", 8 * b, 8 * b + 8)
                for b in range(NB):
                    mm(b, "RP", 128 * b, "CA", 0)
                for b in range(NB):
                    winner(b, 128, G * pair[0])
                cp(ix, ("WL", 0, 4 * NB, 4))
            else:
                m, far = ("MX%d" % t, 0, NB), _far(rank, t, T, topo)
                for b in range(NB):
                    mm(b, "RP", 128 * b, "CM%d" % t, CA_)
                for b in range(NB):
                    i, o = ("PS", 512 * b, 512 * b + 2 * G), ("MX%d" % t, b, b + 1)
                    op("v", lambda v, i=i, o=o: v.tensor_reduce(view(o), view(i), AX, AL.max), [i], [o])
                for i, r in enumerate(far):
                    send([(efar, "aM%d%d" % (t, i), m, [(T.cores[r], ("MR%d" % t, 8 * i, 8 * i + NB))])])
                for b in range(NB):
                    winner(b, 2 * G, 0)
                old(t)
                numbers(t - 1)
                results(t - 1)
                for i, r in enumerate(far[::-1]):
                    tt(("CP", 1 + i, 4 * NB, 4), m, ("MR%d" % t, 8 * i, 8 * i + NB), AL.is_gt if r < rank else AL.is_ge)
                scan(("PR", 0, 4 * NB), ("CP", 0, 4 * NB), ("WL", 0, 4 * NB), 0.0, AL.mult, AL.add)
                cp(ix, ("PR", 3, 4 * NB, 4))
            if final:
                send([(eall, "aL%d" % t, ix, [(T.cores[mate], ("IY", 0, NB))])])
                wait("y", (done["v"], cnt["v"] + 3))
                stores(t - 1)
                admit(t, ix, [me])
            else:
                if t > 0:
                    wait("y", (done["v"], cnt["v"]))
                    stores(t - 1)
                admit(t, ix, [1 - me, me])
            flags(n, final)
            move(t)
            if not final:
                for k in "cs":
                    x = ("CM%d%s" % (t + 1, k), co, co + G)
                    send([(eall, "aN%d" % (t + 1), x, [(T.cores[mate], x)])])
                ts(("YL", 0, 1), qc, ("FF", 1, 2), AL.add)
                ts(("IL", 0, 4, 2), n, float(Z), AL.add)
        else:
            if t > 0:
                blank(t)
                old(t)
                numbers(t - 1)
                results(t - 1)
                stores(t - 1)
            if final:
                admit(t, ("IY", 0, NB), [me])
                flags(n, True)
            else:
                nx = "TK%d" % (t + 1)
                blank(t + 1)
                qz(nx, 128 * rank, 128, "X12", 4 * TOK * t)
                if t + 2 == R:
                    for k in "cs":
                        es, w = share[k]
                        send([(es[w * i:w * i + w], "aT%s%d" % (k, t + 1), tokens(t + 1, k, r), [(T.cores[mate], tokens(t + 1, k, r))])
                              for i, r in enumerate([r for r in range(NR) if r != mate])])
                else:
                    qz("TK%d" % (R - 1), 128 * rank, 128, "X12", 4 * TOK * (R - 2))
                for a in (0, 4 * NB):
                    pickc("RP", 16 * a, nx, 0, Z + 128, "RL", a, a + 4 * NB)
                for q, a in (("s", 0), ("v", 4 * NB)):
                    picks(q, "RP", 16 * a, nx, 0, Z + 128, "RL", a, a + 4 * NB)
                flags(("LN%d" % t, 0, 2), True)
            move(t)
    hn = "CM%d" % R
    i = (hn + "c", co, co + G)
    dma("y", T.oc[:, 0:4 * G], view(i).bitcast(dt.uint8), [i], [])
    for k in range(4):
        dma("ssys"[k], T.osc[4 * k:4 * k + 4, 0:G], T[hn + "s"][32 * k:32 * k + 4, co:co + G], [(hn + "s", co, co + G)], [])

    for tok in outer:
        wait("g", tok)
    g.wait_ge(T.sem.sent, sent[0])
    for q in cnt:
        wait("g", (done[q], cnt[q]))
    for i in range(nd[0]):
        wait("g", ("d%d" % i, 16))
